import numpy as np
import ml_dtypes


def mxq(x, axis, fmt="e4m3"):
    dtype, down = {"e4m3": (ml_dtypes.float8_e4m3fn, 7), "e5m2": (ml_dtypes.float8_e5m2, 14)}[fmt]
    v = np.moveaxis(np.asarray(x, np.float32).astype(ml_dtypes.bfloat16).astype(np.float64), axis, -1)
    blocks = v.reshape(v.shape[:-1] + (-1, 32))
    amax = np.abs(blocks).max(-1, keepdims=True)
    byte = np.maximum(np.where(amax > 0, np.frexp(amax)[1] - 1 + 127, 0) - down, 1)
    scale = np.exp2(byte - 127.0)
    codes = (blocks / scale).astype(np.float32).astype(dtype).astype(np.float64)
    return np.moveaxis((codes * scale).reshape(v.shape), -1, axis)


WIDE = False


def mx_kscale(k):
    if not WIDE:
        return np.ones(k)
    levels = np.array([10, -10, 5, -5, 0])
    if k % 512:
        return np.exp2(np.random.permutation(np.resize(levels, k // 32))).repeat(32)
    a = np.empty((k // 512, 16))
    for p in range(k // 512):
        a[p, :8] = np.random.permutation(np.resize(levels, 8))
        for g in range(8):
            far = levels[np.abs(levels - a[p, g]) >= 10]
            a[p, g + 8] = far[np.random.randint(len(far))]
    return np.exp2(a.ravel()).repeat(32)


def f64(x):
    return np.asarray(x).astype(np.float64)


def striped(idx):
    return np.tile(idx.reshape(-1, 16).T, (8, 1)).astype(np.uint16)


def unstriped(offs):
    return offs[:16].T.reshape(-1).astype(np.int64)


E2M1 = np.array([0.0, 0.5, 1.0, 1.5, 2.0, 3.0, 4.0, 6.0, -0.0, -0.5, -1.0, -1.5, -2.0, -3.0, -4.0, -6.0])


def pack_fp4(w):
    k, n = w.shape
    w = f64(np.asarray(w, np.float32).astype(ml_dtypes.bfloat16)).reshape(k // 32, 32, n)
    amax = np.abs(w).max(1)
    mant, ex = np.frexp(amax / 6.0)
    byte = np.clip(np.where(amax > 0, np.where(mant > 0.5, ex, ex - 1) + 127, 1), 1, 254)
    scaled = (w * np.exp2(127.0 - byte)[:, None, :]).reshape(k, n).astype(np.float32)
    c = np.ascontiguousarray(scaled.reshape(k // 512, 128, 4, n).transpose(0, 1, 3, 2)).astype(ml_dtypes.float4_e2m1fn).view(np.uint8) & 0xF
    words = (c[..., 0::2] | (c[..., 1::2] << 4)).reshape(k // 512, 128, 2 * n)
    return np.ascontiguousarray(words), np.ascontiguousarray(byte.astype(np.uint8).reshape(k // 512, 16, n))


def unpack_fp4(words, scales):
    g, _, n = scales.shape
    words = np.ascontiguousarray(words).reshape(g, 128, n, 2)
    nib = np.empty((g, 128, n, 4), np.uint8)
    nib[..., 0::2] = words & 0xF
    nib[..., 1::2] = words >> 4
    vals = E2M1[nib] * np.repeat(np.exp2(scales.astype(np.float64) - 127.0), 8, axis=1)[..., None]
    return vals.transpose(0, 1, 3, 2).reshape(g * 512, n)


K, T, S, V, N = 512, 2048, 1024, 512, 256


def setup_inputs():
    n = np.random.standard_normal
    s = mx_kscale(K)[:, None]
    packed_w1 = pack_fp4(n((K, N)) / np.sqrt(K) / s)
    return {
        "xT": (n((K, T)) * s).astype(np.float32),
        "w1_words": packed_w1[0],
        "w1_scales": packed_w1[1],
        "offs": striped(np.random.permutation(T)[:S]),
        "pos1": striped(np.random.permutation(S)[:V]),
        "pos2": striped(np.random.permutation(S)[:V]),
        "pos3": striped(np.random.permutation(S)[:V]),
    }


def reference(xT, w1_words, w1_scales, offs, pos1, pos2, pos3):
    xq = mxq(f64(xT)[:, unstriped(offs)], 0, "e4m3")
    y = unpack_fp4(w1_words, w1_scales).T @ xq
    n0 = y[:, unstriped(pos1)]
    n1 = y[:, unstriped(pos2)]
    n2 = y[:, unstriped(pos3)]
    return np.maximum(np.minimum(n0, n1), np.minimum(np.maximum(n0, n1), n2))

@@ -1,0 +1,144 @@
+from contextlib import ExitStack
+
+import concourse.mybir as mybir
+
+K, T, S, V, N = 512, 2048, 1024, 512, 256
+FLOPS = 2 * K * S * N
+
+F32 = mybir.dt.float32
+BF16 = mybir.dt.bfloat16
+I32 = mybir.dt.int32
+U32 = mybir.dt.uint32
+U16 = mybir.dt.uint16
+U8 = mybir.dt.uint8
+FP8X4 = mybir.dt.float8_e4m3fn_x4
+FP4X4 = mybir.dt.float4_e2m1fn_x4
+MAX = mybir.AluOpType.max
+MIN = mybir.AluOpType.min
+
+P = 128
+LANES = 16
+PIECE = 256
+PIECES = S // PIECE
+
+LOADS = (
+    (0, (("vector", 1024),)),
+    (0, (("vector", 640), ("scalar", 384))),
+    (1, (("scalar", 768),)),
+    (1, (("vector", 640),)),
+    (1, (("scalar", 384),)),
+    (1, (("vector", 256),)),
+)
+
+
+def tile_picked_median_none_e_kernel(tc, xT, w1_words, w1_scales, offs, pos1, pos2, pos3, out):
+    nc = tc.nc
+    with ExitStack() as ctx:
+        keep = ctx.enter_context(tc.tile_pool(name="keep", bufs=1))
+        psum = ctx.enter_context(tc.psum_pool(name="psum", bufs=1))
+
+        x_rows = xT.rearrange("(p j) t -> p j t", j=4)
+        picks = keep.tile([P, S // LANES], U16, name="picks")
+        places = [keep.tile([P, V // LANES], U16, name=f"places{d}") for d in range(3)]
+        w_words = keep.tile([P, 2 * N], U8, name="w_words", align_bytes=64)
+        w_scales = keep.tile([P, N], U8, name="w_scales", align_bytes=64)
+
+        nc.gpsimd.memset(w_scales[:], 0)
+        for q in range(4):
+            nc.gpsimd.dma_start(out=w_scales[32 * q : 32 * q + 4, :].bitcast(I32), in_=w1_scales[0, 4 * q : 4 * q + 4, :].bitcast(I32))
+
+        raws = []
+        done = [0, 0]
+        for i, (u, shares) in enumerate(LOADS):
+            width = sum(w for e, w in shares)
+            raw = keep.tile([P, 2, width], F32, name=f"raw{i}")
+            nc.sync.dma_start(out=raw[:], in_=x_rows[:, 2 * u : 2 * u + 2, done[u] : done[u] + width])
+            raws.append((raw, done[u]))
+            done[u] = done[u] + width
+            if i == 0:
+                nc.sync.dma_start(picks[:], offs)
+        nc.sync.dma_start(out=w_words[:], in_=w1_words[0])
+        for place, pos in zip(places, (pos1, pos2, pos3)):
+            nc.sync.dma_start(place[:], pos)
+
+        pairs = [keep.tile([P, T, 2], BF16, name=f"pairs{u}", align_bytes=64) for u in range(2)]
+        picked = [keep.tile([P, 2, PIECE], U32, name=f"picked{q}") for q in range(PIECES)]
+
+        def round_pairs(u):
+            for (lu, shares), (raw, c0) in zip(LOADS, raws):
+                if lu != u:
+                    continue
+                a = 0
+                for engine, w in shares:
+                    src = raw[:, :, a : a + w].rearrange("p j c -> p c j")
+                    dst = pairs[u][:, c0 + a : c0 + a + w, :]
+                    if engine == "vector":
+                        nc.vector.tensor_copy(out=dst, in_=src)
+                    else:
+                        nc.scalar.copy(out=dst, in_=src)
+                    a = a + w
+
+        def gather_pairs(u):
+            window = pairs[u][:].rearrange("p t e -> p (t e)").bitcast(U32)
+            for q in range(PIECES):
+                cols = slice(q * PIECE // LANES, (q + 1) * PIECE // LANES)
+                nc.vector.tensor_copy(out=picked[q][:, u, :], in_=window.indirect(picks[:, cols]))
+
+        round_pairs(0)
+        gather_pairs(0)
+        round_pairs(1)
+        gather_pairs(1)
+
+        codes = keep.tile([P, S], U32, name="codes", align_bytes=64)
+        scales = keep.tile([P, S], U8, name="scales", align_bytes=64)
+        ys = [keep.tile([P, S], F32, name=f"y{b}") for b in range(2)]
+
+        def product(b, c0, width, tag):
+            acc = psum.tile([P, 512], F32, name=f"acc{b}_{c0}", tag=tag)
+            nc.tensor.matmul_mx(
+                out=acc[:, 0:width],
+                lhsT=w_words[:, 2 * P * b : 2 * P * (b + 1)].bitcast(FP4X4),
+                lhsT_scale=w_scales[:, P * b : P * (b + 1)],
+                rhs=codes[:, c0 : c0 + width].bitcast(FP8X4),
+                rhs_scale=scales[:, c0 : c0 + width],
+                start=True,
+                stop=True,
+            )
+            nc.scalar.copy(out=ys[b][:, c0 : c0 + width], in_=acc[:, 0:width])
+
+        woven = []
+        for q in range(PIECES):
+            quad = keep.tile([P, PIECE, 2], U32, name=f"quad{q}", align_bytes=64)
+            nc.scalar.copy(out=quad[:], in_=picked[q][:].rearrange("p u n -> p n u"))
+            woven.append(quad)
+        for q in range(PIECES):
+            cols = slice(q * PIECE, (q + 1) * PIECE)
+            nc.vector.quantize_mx(
+                out=codes[:, cols].bitcast(FP8X4),
+                scales=scales[:, cols],
+                in_=woven[q][:].rearrange("p n u -> p (n u)").bitcast(BF16),
+            )
+            product(0, q * PIECE, PIECE, f"bank{q}")
+        product(1, 0, 512, "bank3")
+        product(1, 512, 512, "bank2")
+
+        def neighbours(b, d):
+            got = keep.tile([P, V], F32, name=f"n{b}_{d}")
+            nc.vector.tensor_copy(out=got[:], in_=ys[b][:].indirect(places[d][:]))
+            return got
+
+        for b in range(2):
+            n0, n1, n2 = (neighbours(b, d) for d in range(3))
+            hi = keep.tile([P, V], F32, name=f"hi{b}")
+            lo = keep.tile([P, V], F32, name=f"lo{b}")
+            cap = keep.tile([P, V], F32, name=f"cap{b}")
+            nc.vector.tensor_tensor(hi[:], n0[:], n1[:], MAX)
+            nc.vector.tensor_tensor(lo[:], n0[:], n1[:], MIN)
+            parts = (slice(0, V),) if b == 0 else (slice(0, 256), slice(256, V))
+            for cols in parts:
+                nc.vector.tensor_tensor(cap[:, cols], hi[:, cols], n2[:, cols], MIN)
+            for i, cols in enumerate(parts):
+                med = keep.tile([P, cols.stop - cols.start], F32, name=f"med{b}_{i}")
+                nc.vector.tensor_tensor(med[:], lo[:, cols], cap[:, cols], MAX)
+                queue = nc.scalar if i == 1 else nc.sync
+                queue.dma_start(out=out[P * b : P * (b + 1), cols], in_=med[:])

@@ -21,13 +21,15 @@ LANES = 16
 PIECE = 256
 PIECES = S // PIECE
 
+STRETCHES = ((0, 256), (256, 256), (512, 256), (768, 128), (896, 128))
 LOADS = (
     (0, (("vector", 1024),)),
-    (0, (("vector", 640), ("scalar", 384))),
+    (0, (("vector", 384), ("scalar", 384))),
+    (0, (("vector", 256),)),
     (1, (("scalar", 768),)),
-    (1, (("vector", 640),)),
-    (1, (("scalar", 384),)),
-    (1, (("vector", 256),)),
+    (1, (("vector", 768),)),
+    (1, (("scalar", 320),)),
+    (1, (("vector", 192),)),
 )
 
 
@@ -43,9 +45,7 @@ def tile_picked_median_none_e_kernel(tc, xT, w1_words, w1_scales, offs, pos1, po
         w_words = keep.tile([P, 2 * N], U8, name="w_words", align_bytes=64)
         w_scales = keep.tile([P, N], U8, name="w_scales", align_bytes=64)
 
-        nc.gpsimd.memset(w_scales[:], 0)
-        for q in range(4):
-            nc.gpsimd.dma_start(out=w_scales[32 * q : 32 * q + 4, :].bitcast(I32), in_=w1_scales[0, 4 * q : 4 * q + 4, :].bitcast(I32))
+        nc.vector.memset(w_scales[:].bitcast(I32), 0)
 
         raws = []
         done = [0, 0]
@@ -58,6 +58,8 @@ def tile_picked_median_none_e_kernel(tc, xT, w1_words, w1_scales, offs, pos1, po
             if i == 0:
                 nc.sync.dma_start(picks[:], offs)
         nc.sync.dma_start(out=w_words[:], in_=w1_words[0])
+        for q in range(4):
+            nc.sync.dma_start(out=w_scales[32 * q : 32 * q + 4, :].bitcast(I32), in_=w1_scales[0, 4 * q : 4 * q + 4, :].bitcast(I32))
         for place, pos in zip(places, (pos1, pos2, pos3)):
             nc.sync.dma_start(place[:], pos)
 
@@ -107,38 +109,48 @@ def tile_picked_median_none_e_kernel(tc, xT, w1_words, w1_scales, offs, pos1, po
             nc.scalar.copy(out=ys[b][:, c0 : c0 + width], in_=acc[:, 0:width])
 
         woven = []
-        for q in range(PIECES):
-            quad = keep.tile([P, PIECE, 2], U32, name=f"quad{q}", align_bytes=64)
-            nc.scalar.copy(out=quad[:], in_=picked[q][:].rearrange("p u n -> p n u"))
+        for i, (c0, width) in enumerate(STRETCHES):
+            quad = keep.tile([P, width, 2], U32, name=f"quad{i}", align_bytes=64)
+            a = c0 % PIECE
+            nc.scalar.copy(out=quad[:], in_=picked[c0 // PIECE][:, :, a : a + width].rearrange("p u n -> p n u"))
             woven.append(quad)
-        for q in range(PIECES):
-            cols = slice(q * PIECE, (q + 1) * PIECE)
+        for i, (c0, width) in enumerate(STRETCHES):
+            cols = slice(c0, c0 + width)
             nc.vector.quantize_mx(
                 out=codes[:, cols].bitcast(FP8X4),
                 scales=scales[:, cols],
-                in_=woven[q][:].rearrange("p n u -> p (n u)").bitcast(BF16),
+                in_=woven[i][:].rearrange("p n u -> p (n u)").bitcast(BF16),
             )
-            product(0, q * PIECE, PIECE, f"bank{q}")
-        product(1, 0, 512, "bank3")
-        product(1, 512, 512, "bank2")
+            product(0, c0, width, f"bank{i}")
+        product(1, 0, 512, "bank4")
+        product(1, 512, 512, "bank3")
 
-        def neighbours(b, d):
-            got = keep.tile([P, V], F32, name=f"n{b}_{d}")
-            nc.vector.tensor_copy(out=got[:], in_=ys[b][:].indirect(places[d][:]))
-            return got
+        def gather(got, b, d, cols):
+            entries = places[d][:, cols.start // LANES : cols.stop // LANES]
+            nc.vector.tensor_copy(out=got[:, cols], in_=ys[b][:].indirect(entries))
 
+        def finish(b, lo, cap, cols, queue):
+            med = keep.tile([P, cols.stop - cols.start], F32, name=f"med{b}_{cols.start}")
+            nc.vector.tensor_tensor(med[:], lo[:, cols], cap[:, cols], MAX)
+            queue.dma_start(out=out[P * b : P * (b + 1), cols], in_=med[:])
+
+        whole = slice(0, V)
         for b in range(2):
-            n0, n1, n2 = (neighbours(b, d) for d in range(3))
-            hi = keep.tile([P, V], F32, name=f"hi{b}")
-            lo = keep.tile([P, V], F32, name=f"lo{b}")
-            cap = keep.tile([P, V], F32, name=f"cap{b}")
+            n0, n1, n2, hi, lo, cap = (keep.tile([P, V], F32, name=f"{what}_{b}") for what in ("n0", "n1", "n2", "hi", "lo", "cap"))
+            head = whole if b == 0 else slice(0, 256)
+            gather(n0, b, 0, whole)
+            gather(n1, b, 1, whole)
+            gather(n2, b, 2, head)
             nc.vector.tensor_tensor(hi[:], n0[:], n1[:], MAX)
             nc.vector.tensor_tensor(lo[:], n0[:], n1[:], MIN)
-            parts = (slice(0, V),) if b == 0 else (slice(0, 256), slice(256, V))
-            for cols in parts:
-                nc.vector.tensor_tensor(cap[:, cols], hi[:, cols], n2[:, cols], MIN)
-            for i, cols in enumerate(parts):
-                med = keep.tile([P, cols.stop - cols.start], F32, name=f"med{b}_{i}")
-                nc.vector.tensor_tensor(med[:], lo[:, cols], cap[:, cols], MAX)
-                queue = nc.scalar if i == 1 else nc.sync
-                queue.dma_start(out=out[P * b : P * (b + 1), cols], in_=med[:])
+            nc.vector.tensor_tensor(cap[:, head], hi[:, head], n2[:, head], MIN)
+            if b == 0:
+                finish(b, lo, cap, head, nc.sync)
+            else:
+                gather(n2, b, 2, slice(256, V))
+                finish(b, lo, cap, head, nc.sync)
+                ends = (slice(256, 384), slice(384, V))
+                for cols in ends:
+                    nc.vector.tensor_tensor(cap[:, cols], hi[:, cols], n2[:, cols], MIN)
+                for cols, queue in zip(ends, (nc.scalar, nc.sync)):
+                    finish(b, lo, cap, cols, queue)

@@ -23,13 +23,14 @@ PIECES = S // PIECE
 
 STRETCHES = ((0, 256), (256, 256), (512, 256), (768, 128), (896, 128))
 LOADS = (
-    (0, (("vector", 1024),)),
-    (0, (("vector", 384), ("scalar", 384))),
-    (0, (("vector", 256),)),
-    (1, (("scalar", 768),)),
-    (1, (("vector", 768),)),
-    (1, (("scalar", 320),)),
-    (1, (("vector", 192),)),
+    (0, (("vector", 640), ("scalar", 384))),
+    (0, (("vector", 320), ("scalar", 192))),
+    (0, (("vector", 336), ("scalar", 176))),
+    (1, (("scalar", 512),)),
+    (1, (("scalar", 384), ("vector", 128))),
+    (1, (("vector", 384), ("scalar", 128))),
+    (1, (("vector", 160), ("scalar", 96))),
+    (1, (("vector", 168), ("scalar", 88))),
 )
 
 
@@ -106,7 +107,10 @@ def tile_picked_median_none_e_kernel(tc, xT, w1_words, w1_scales, offs, pos1, po
                 start=True,
                 stop=True,
             )
-            nc.scalar.copy(out=ys[b][:, c0 : c0 + width], in_=acc[:, 0:width])
+            if b == 0 and c0 in (256, 768):
+                nc.vector.tensor_copy(out=ys[b][:, c0 : c0 + width], in_=acc[:, 0:width])
+            else:
+                nc.scalar.copy(out=ys[b][:, c0 : c0 + width], in_=acc[:, 0:width])
 
         woven = []
         for i, (c0, width) in enumerate(STRETCHES):
@@ -122,8 +126,8 @@ def tile_picked_median_none_e_kernel(tc, xT, w1_words, w1_scales, offs, pos1, po
                 in_=woven[i][:].rearrange("p n u -> p (n u)").bitcast(BF16),
             )
             product(0, c0, width, f"bank{i}")
-        product(1, 0, 512, "bank4")
-        product(1, 512, 512, "bank3")
+        product(1, 0, 512, "bank3")
+        product(1, 512, 512, "bank4")
 
         def gather(got, b, d, cols):
             entries = places[d][:, cols.start // LANES : cols.stop // LANES]

@@ -15,23 +15,20 @@ FP8X4 = mybir.dt.float8_e4m3fn_x4
 FP4X4 = mybir.dt.float4_e2m1fn_x4
 MAX = mybir.AluOpType.max
 MIN = mybir.AluOpType.min
+COPY = mybir.ActivationFunctionType.Copy
 
 P = 128
 LANES = 16
-PIECE = 256
-PIECES = S // PIECE
 
-STRETCHES = ((0, 256), (256, 256), (512, 256), (768, 128), (896, 128))
-LOADS = (
-    (0, (("vector", 640), ("scalar", 384))),
-    (0, (("vector", 320), ("scalar", 192))),
-    (0, (("vector", 336), ("scalar", 176))),
-    (1, (("scalar", 512),)),
-    (1, (("scalar", 384), ("vector", 128))),
-    (1, (("vector", 384), ("scalar", 128))),
-    (1, (("vector", 160), ("scalar", 96))),
-    (1, (("vector", 168), ("scalar", 88))),
+CHUNKS = (
+    ((1024, "scalar"), (1024, "vector"),),
+    ((1024, "vector"), (1024, "vector"),),
+    ((1024, "vector"), (512, "vector"), (512, "vector"),),
+    ((1024, "vector"), (512, "vector"), (512, "vector"),),
 )
+VECTOR_PIECES = ((384, 384),)
+SCALAR_PIECES = ((0, 384), (768, 256))
+STRETCHES = ((512, 256), (0, 256), (256, 256), (768, 128), (896, 128))
 
 
 def tile_picked_median_none_e_kernel(tc, xT, w1_words, w1_scales, offs, pos1, pos2, pos3, out):
@@ -48,55 +45,45 @@ def tile_picked_median_none_e_kernel(tc, xT, w1_words, w1_scales, offs, pos1, po
 
         nc.vector.memset(w_scales[:].bitcast(I32), 0)
 
-        raws = []
-        done = [0, 0]
-        for i, (u, shares) in enumerate(LOADS):
-            width = sum(w for e, w in shares)
-            raw = keep.tile([P, 2, width], F32, name=f"raw{i}")
-            nc.sync.dma_start(out=raw[:], in_=x_rows[:, 2 * u : 2 * u + 2, done[u] : done[u] + width])
-            raws.append((raw, done[u]))
-            done[u] = done[u] + width
-            if i == 0:
-                nc.sync.dma_start(picks[:], offs)
+        raws = [keep.tile([P, T], F32, name=f"raw{t}") for t in range(4)]
+        rounded = [keep.tile([P, T], BF16, name=f"rounded{t}") for t in range(4)]
+        for t in range(4):
+            c0 = 0
+            for width, engine in CHUNKS[t]:
+                nc.sync.dma_start(out=raws[t][:, c0 : c0 + width], in_=x_rows[:, t, c0 : c0 + width])
+                if t == 0 and c0 == 0:
+                    nc.sync.dma_start(picks[:], offs)
+                c0 = c0 + width
         nc.sync.dma_start(out=w_words[:], in_=w1_words[0])
         for q in range(4):
             nc.sync.dma_start(out=w_scales[32 * q : 32 * q + 4, :].bitcast(I32), in_=w1_scales[0, 4 * q : 4 * q + 4, :].bitcast(I32))
         for place, pos in zip(places, (pos1, pos2, pos3)):
             nc.sync.dma_start(place[:], pos)
 
-        pairs = [keep.tile([P, T, 2], BF16, name=f"pairs{u}", align_bytes=64) for u in range(2)]
-        picked = [keep.tile([P, 2, PIECE], U32, name=f"picked{q}") for q in range(PIECES)]
+        quads = keep.tile([P, 4 * S], BF16, name="quads", align_bytes=64)
+        slots = quads[:].rearrange("p (n t) -> p n t", t=4)
 
-        def round_pairs(u):
-            for (lu, shares), (raw, c0) in zip(LOADS, raws):
-                if lu != u:
-                    continue
-                a = 0
-                for engine, w in shares:
-                    src = raw[:, :, a : a + w].rearrange("p j c -> p c j")
-                    dst = pairs[u][:, c0 + a : c0 + a + w, :]
-                    if engine == "vector":
-                        nc.vector.tensor_copy(out=dst, in_=src)
-                    else:
-                        nc.scalar.copy(out=dst, in_=src)
-                    a = a + w
-
-        def gather_pairs(u):
-            window = pairs[u][:].rearrange("p t e -> p (t e)").bitcast(U32)
-            for q in range(PIECES):
-                cols = slice(q * PIECE // LANES, (q + 1) * PIECE // LANES)
-                nc.vector.tensor_copy(out=picked[q][:, u, :], in_=window.indirect(picks[:, cols]))
-
-        round_pairs(0)
-        gather_pairs(0)
-        round_pairs(1)
-        gather_pairs(1)
+        for t in range(4):
+            c0 = 0
+            for width, engine in CHUNKS[t]:
+                cols = slice(c0, c0 + width)
+                if engine == "vector":
+                    nc.vector.tensor_copy(out=rounded[t][:, cols], in_=raws[t][:, cols])
+                else:
+                    nc.scalar.copy(out=rounded[t][:, cols], in_=raws[t][:, cols])
+                c0 = c0 + width
+            for e0, count in VECTOR_PIECES:
+                entries = picks[:, e0 // LANES : (e0 + count) // LANES]
+                nc.vector.tensor_copy(out=slots[:, e0 : e0 + count, t], in_=raws[t][:].indirect(entries))
+            for e0, count in SCALAR_PIECES:
+                entries = picks[:, e0 // LANES : (e0 + count) // LANES]
+                nc.scalar.activation(slots[:, e0 : e0 + count, t], rounded[t][:].indirect(entries), COPY)
 
         codes = keep.tile([P, S], U32, name="codes", align_bytes=64)
         scales = keep.tile([P, S], U8, name="scales", align_bytes=64)
         ys = [keep.tile([P, S], F32, name=f"y{b}") for b in range(2)]
 
-        def product(b, c0, width, tag):
+        def product(b, c0, width, tag, engine):
             acc = psum.tile([P, 512], F32, name=f"acc{b}_{c0}", tag=tag)
             nc.tensor.matmul_mx(
                 out=acc[:, 0:width],
@@ -107,27 +94,22 @@ def tile_picked_median_none_e_kernel(tc, xT, w1_words, w1_scales, offs, pos1, po
                 start=True,
                 stop=True,
             )
-            if b == 0 and c0 in (256, 768):
+            if engine == "vector":
                 nc.vector.tensor_copy(out=ys[b][:, c0 : c0 + width], in_=acc[:, 0:width])
             else:
                 nc.scalar.copy(out=ys[b][:, c0 : c0 + width], in_=acc[:, 0:width])
 
-        woven = []
-        for i, (c0, width) in enumerate(STRETCHES):
-            quad = keep.tile([P, width, 2], U32, name=f"quad{i}", align_bytes=64)
-            a = c0 % PIECE
-            nc.scalar.copy(out=quad[:], in_=picked[c0 // PIECE][:, :, a : a + width].rearrange("p u n -> p n u"))
-            woven.append(quad)
         for i, (c0, width) in enumerate(STRETCHES):
             cols = slice(c0, c0 + width)
             nc.vector.quantize_mx(
                 out=codes[:, cols].bitcast(FP8X4),
                 scales=scales[:, cols],
-                in_=woven[i][:].rearrange("p n u -> p (n u)").bitcast(BF16),
+                in_=quads[:, 4 * c0 : 4 * (c0 + width)],
             )
-            product(0, c0, width, f"bank{i}")
-        product(1, 0, 512, "bank3")
-        product(1, 512, 512, "bank4")
+        for i, (c0, width) in enumerate(STRETCHES):
+            product(0, c0, width, f"bank{i}", "vector" if i >= 3 else "scalar")
+        product(1, 0, 512, "bank3", "scalar")
+        product(1, 512, 512, "bank4", "scalar")
 
         def gather(got, b, d, cols):
             entries = places[d][:, cols.start // LANES : cols.stop // LANES]
@@ -139,22 +121,23 @@ def tile_picked_median_none_e_kernel(tc, xT, w1_words, w1_scales, offs, pos1, po
             queue.dma_start(out=out[P * b : P * (b + 1), cols], in_=med[:])
 
         whole = slice(0, V)
-        for b in range(2):
-            n0, n1, n2, hi, lo, cap = (keep.tile([P, V], F32, name=f"{what}_{b}") for what in ("n0", "n1", "n2", "hi", "lo", "cap"))
-            head = whole if b == 0 else slice(0, 256)
-            gather(n0, b, 0, whole)
-            gather(n1, b, 1, whole)
-            gather(n2, b, 2, head)
-            nc.vector.tensor_tensor(hi[:], n0[:], n1[:], MAX)
-            nc.vector.tensor_tensor(lo[:], n0[:], n1[:], MIN)
-            nc.vector.tensor_tensor(cap[:, head], hi[:, head], n2[:, head], MIN)
-            if b == 0:
-                finish(b, lo, cap, head, nc.sync)
-            else:
-                gather(n2, b, 2, slice(256, V))
-                finish(b, lo, cap, head, nc.sync)
-                ends = (slice(256, 384), slice(384, V))
-                for cols in ends:
-                    nc.vector.tensor_tensor(cap[:, cols], hi[:, cols], n2[:, cols], MIN)
-                for cols, queue in zip(ends, (nc.scalar, nc.sync)):
-                    finish(b, lo, cap, cols, queue)
+        n0, n1, n2, hi, lo, cap = ([keep.tile([P, V], F32, name=f"{what}_{b}") for b in range(2)] for what in ("n0", "n1", "n2", "hi", "lo", "cap"))
+        gather(n0[0], 0, 0, whole)
+        gather(n1[0], 0, 1, whole)
+        gather(n2[0], 0, 2, whole)
+        nc.vector.tensor_tensor(hi[0][:], n0[0][:], n1[0][:], MAX)
+        nc.vector.tensor_tensor(lo[0][:], n0[0][:], n1[0][:], MIN)
+        nc.vector.tensor_tensor(cap[0][:], hi[0][:], n2[0][:], MIN)
+        gather(n0[1], 1, 0, whole)
+        finish(0, lo[0], cap[0], whole, nc.sync)
+        gather(n1[1], 1, 1, whole)
+        gather(n2[1], 1, 2, whole)
+        nc.vector.tensor_tensor(hi[1][:], n0[1][:], n1[1][:], MAX)
+        nc.vector.tensor_tensor(lo[1][:], n0[1][:], n1[1][:], MIN)
+        ends = (slice(0, 256), slice(256, 384), slice(384, V))
+        for cols in ends[:2]:
+            nc.vector.tensor_tensor(cap[1][:, cols], hi[1][:, cols], n2[1][:, cols], MIN)
+        finish(1, lo[1], cap[1], ends[0], nc.sync)
+        nc.vector.tensor_tensor(cap[1][:, ends[2]], hi[1][:, ends[2]], n2[1][:, ends[2]], MIN)
+        finish(1, lo[1], cap[1], ends[1], nc.scalar)
+        finish(1, lo[1], cap[1], ends[2], nc.sync)

@@ -20,14 +20,15 @@ COPY = mybir.ActivationFunctionType.Copy
 P = 128
 LANES = 16
 
+LOAD_ORDER = (2, 0, 1, 3)
 CHUNKS = (
     ((1024, "scalar"), (1024, "vector"),),
     ((1024, "vector"), (1024, "vector"),),
     ((1024, "vector"), (512, "vector"), (512, "vector"),),
     ((1024, "vector"), (512, "vector"), (512, "vector"),),
 )
-VECTOR_PIECES = ((384, 384),)
-SCALAR_PIECES = ((0, 384), (768, 256))
+VECTOR_SHARE = (320, 320, 384, 384)
+LAST_PIECE = 256
 STRETCHES = ((512, 256), (0, 256), (256, 256), (768, 128), (896, 128))
 
 
@@ -47,11 +48,11 @@ def tile_picked_median_none_e_kernel(tc, xT, w1_words, w1_scales, offs, pos1, po
 
         raws = [keep.tile([P, T], F32, name=f"raw{t}") for t in range(4)]
         rounded = [keep.tile([P, T], BF16, name=f"rounded{t}") for t in range(4)]
-        for t in range(4):
+        for chunks, t in zip(CHUNKS, LOAD_ORDER):
             c0 = 0
-            for width, engine in CHUNKS[t]:
+            for width, engine in chunks:
                 nc.sync.dma_start(out=raws[t][:, c0 : c0 + width], in_=x_rows[:, t, c0 : c0 + width])
-                if t == 0 and c0 == 0:
+                if t == LOAD_ORDER[0] and c0 == 0:
                     nc.sync.dma_start(picks[:], offs)
                 c0 = c0 + width
         nc.sync.dma_start(out=w_words[:], in_=w1_words[0])
@@ -63,19 +64,19 @@ def tile_picked_median_none_e_kernel(tc, xT, w1_words, w1_scales, offs, pos1, po
         quads = keep.tile([P, 4 * S], BF16, name="quads", align_bytes=64)
         slots = quads[:].rearrange("p (n t) -> p n t", t=4)
 
-        for t in range(4):
+        for chunks, t in zip(CHUNKS, LOAD_ORDER):
             c0 = 0
-            for width, engine in CHUNKS[t]:
+            for width, engine in chunks:
                 cols = slice(c0, c0 + width)
                 if engine == "vector":
                     nc.vector.tensor_copy(out=rounded[t][:, cols], in_=raws[t][:, cols])
                 else:
                     nc.scalar.copy(out=rounded[t][:, cols], in_=raws[t][:, cols])
                 c0 = c0 + width
-            for e0, count in VECTOR_PIECES:
+            for e0, count in ((S - LAST_PIECE - VECTOR_SHARE[t], VECTOR_SHARE[t]),):
                 entries = picks[:, e0 // LANES : (e0 + count) // LANES]
                 nc.vector.tensor_copy(out=slots[:, e0 : e0 + count, t], in_=raws[t][:].indirect(entries))
-            for e0, count in SCALAR_PIECES:
+            for e0, count in ((0, S - LAST_PIECE - VECTOR_SHARE[t]), (S - LAST_PIECE, LAST_PIECE)):
                 entries = picks[:, e0 // LANES : (e0 + count) // LANES]
                 nc.scalar.activation(slots[:, e0 : e0 + count, t], rounded[t][:].indirect(entries), COPY)
 

@@ -22,12 +22,12 @@ LANES = 16
 
 LOAD_ORDER = (2, 0, 1, 3)
 CHUNKS = (
-    ((1024, "scalar"), (1024, "vector"),),
-    ((1024, "vector"), (1024, "vector"),),
-    ((1024, "vector"), (512, "vector"), (512, "vector"),),
-    ((1024, "vector"), (512, "vector"), (512, "vector"),),
+    ((1024, "scalar"), (1024, "vector")),
+    ((1024, "gpsimd"), (1024, "vector")),
+    ((512, "gpsimd"), (1024, "vector"), (512, "vector")),
+    ((512, "gpsimd"), (1024, "vector"), (512, "vector")),
 )
-VECTOR_SHARE = (320, 320, 384, 384)
+VECTOR_SHARE = (384, 384, 384, 384)
 LAST_PIECE = 256
 STRETCHES = ((512, 256), (0, 256), (256, 256), (768, 128), (896, 128))
 
@@ -70,6 +70,8 @@ def tile_picked_median_none_e_kernel(tc, xT, w1_words, w1_scales, offs, pos1, po
                 cols = slice(c0, c0 + width)
                 if engine == "vector":
                     nc.vector.tensor_copy(out=rounded[t][:, cols], in_=raws[t][:, cols])
+                elif engine == "gpsimd":
+                    nc.gpsimd.tensor_copy(out=rounded[t][:, cols], in_=raws[t][:, cols])
                 else:
                     nc.scalar.copy(out=rounded[t][:, cols], in_=raws[t][:, cols])
                 c0 = c0 + width
@@ -108,7 +110,7 @@ def tile_picked_median_none_e_kernel(tc, xT, w1_words, w1_scales, offs, pos1, po
                 in_=quads[:, 4 * c0 : 4 * (c0 + width)],
             )
         for i, (c0, width) in enumerate(STRETCHES):
-            product(0, c0, width, f"bank{i}", "vector" if i >= 3 else "scalar")
+            product(0, c0, width, f"bank{i}", "vector" if i in (1, 2) else "scalar")
         product(1, 0, 512, "bank3", "scalar")
         product(1, 512, 512, "bank4", "scalar")
 

@@ -22,14 +22,15 @@ LANES = 16
 
 LOAD_ORDER = (2, 0, 1, 3)
 CHUNKS = (
-    ((1024, "scalar"), (1024, "vector")),
+    ((2048, "both"),),
     ((1024, "gpsimd"), (1024, "vector")),
     ((512, "gpsimd"), (1024, "vector"), (512, "vector")),
-    ((512, "gpsimd"), (1024, "vector"), (512, "vector")),
+    ((512, "gpsimd"), (1024, "vector"), (256, "vector"), (256, "vector")),
 )
-VECTOR_SHARE = (384, 384, 384, 384)
+FIRST_SPLIT = 1280
+VECTOR_SHARE = (384, 384, 448, 448)
 LAST_PIECE = 256
-STRETCHES = ((512, 256), (0, 256), (256, 256), (768, 128), (896, 128))
+STRETCHES = ((0, 256), (512, 256), (256, 256), (768, 128), (896, 128))
 
 
 def tile_picked_median_none_e_kernel(tc, xT, w1_words, w1_scales, offs, pos1, pos2, pos3, out):
@@ -70,6 +71,9 @@ def tile_picked_median_none_e_kernel(tc, xT, w1_words, w1_scales, offs, pos1, po
                 cols = slice(c0, c0 + width)
                 if engine == "vector":
                     nc.vector.tensor_copy(out=rounded[t][:, cols], in_=raws[t][:, cols])
+                elif engine == "both":
+                    nc.vector.tensor_copy(out=rounded[t][:, 0:FIRST_SPLIT], in_=raws[t][:, 0:FIRST_SPLIT])
+                    nc.scalar.copy(out=rounded[t][:, FIRST_SPLIT:T], in_=raws[t][:, FIRST_SPLIT:T])
                 elif engine == "gpsimd":
                     nc.gpsimd.tensor_copy(out=rounded[t][:, cols], in_=raws[t][:, cols])
                 else:
@@ -137,10 +141,8 @@ def tile_picked_median_none_e_kernel(tc, xT, w1_words, w1_scales, offs, pos1, po
         gather(n2[1], 1, 2, whole)
         nc.vector.tensor_tensor(hi[1][:], n0[1][:], n1[1][:], MAX)
         nc.vector.tensor_tensor(lo[1][:], n0[1][:], n1[1][:], MIN)
-        ends = (slice(0, 256), slice(256, 384), slice(384, V))
-        for cols in ends[:2]:
+        ends = (slice(0, 192), slice(192, 384), slice(384, V))
+        for cols in ends:
             nc.vector.tensor_tensor(cap[1][:, cols], hi[1][:, cols], n2[1][:, cols], MIN)
-        finish(1, lo[1], cap[1], ends[0], nc.sync)
-        nc.vector.tensor_tensor(cap[1][:, ends[2]], hi[1][:, ends[2]], n2[1][:, ends[2]], MIN)
-        finish(1, lo[1], cap[1], ends[1], nc.scalar)
-        finish(1, lo[1], cap[1], ends[2], nc.sync)
+        for cols, queue in zip(ends, (nc.sync, nc.scalar, nc.sync)):
+            finish(1, lo[1], cap[1], cols, queue)

@@ -24,11 +24,11 @@ LOAD_ORDER = (2, 0, 1, 3)
 CHUNKS = (
     ((2048, "both"),),
     ((1024, "gpsimd"), (1024, "vector")),
-    ((512, "gpsimd"), (1024, "vector"), (512, "vector")),
-    ((512, "gpsimd"), (1024, "vector"), (256, "vector"), (256, "vector")),
+    ((512, "gpsimd"), (512, "gpsimd"), (1024, "vector")),
+    ((512, "gpsimd"), (512, "gpsimd"), (512, "vector"), (512, "vector")),
 )
 FIRST_SPLIT = 1280
-VECTOR_SHARE = (384, 384, 448, 448)
+VECTOR_SHARE = (416, 416, 416, 416)
 LAST_PIECE = 256
 STRETCHES = ((0, 256), (512, 256), (256, 256), (768, 128), (896, 128))
 

@@ -1,6 +1,7 @@
 from contextlib import ExitStack
 
 import concourse.mybir as mybir
+from concourse.masks import make_identity
 
 K, T, S, V, N = 512, 2048, 1024, 512, 256
 FLOPS = 2 * K * S * N
@@ -15,7 +16,12 @@ FP8X4 = mybir.dt.float8_e4m3fn_x4
 FP4X4 = mybir.dt.float4_e2m1fn_x4
 MAX = mybir.AluOpType.max
 MIN = mybir.AluOpType.min
+ADD = mybir.AluOpType.add
+SUB = mybir.AluOpType.subtract
+MULT = mybir.AluOpType.mult
 COPY = mybir.ActivationFunctionType.Copy
+SIGN = mybir.ActivationFunctionType.Sign
+ABS = mybir.ActivationFunctionType.Abs
 
 P = 128
 LANES = 16
@@ -31,6 +37,9 @@ FIRST_SPLIT = 1280
 VECTOR_SHARE = (416, 416, 416, 416)
 LAST_PIECE = 256
 STRETCHES = ((0, 256), (512, 256), (256, 256), (768, 128), (896, 128))
+SIDE = 256
+TIE_SCALE = 2.0**40
+TIE_BIAS = 2.0**-110
 
 
 def tile_picked_median_none_e_kernel(tc, xT, w1_words, w1_scales, offs, pos1, pos2, pos3, out):
@@ -46,6 +55,12 @@ def tile_picked_median_none_e_kernel(tc, xT, w1_words, w1_scales, offs, pos1, po
         w_scales = keep.tile([P, N], U8, name="w_scales", align_bytes=64)
 
         nc.vector.memset(w_scales[:].bitcast(I32), 0)
+
+        identity = keep.tile([P, P], F32, name="identity")
+        make_identity(nc, identity[:])
+        ties = keep.tile([P, 2], F32, name="ties")
+        nc.gpsimd.memset(ties[:, 0:1], TIE_BIAS)
+        nc.gpsimd.memset(ties[:, 1:2], -TIE_BIAS)
 
         raws = [keep.tile([P, T], F32, name=f"raw{t}") for t in range(4)]
         rounded = [keep.tile([P, T], BF16, name=f"rounded{t}") for t in range(4)]
@@ -118,31 +133,75 @@ def tile_picked_median_none_e_kernel(tc, xT, w1_words, w1_scales, offs, pos1, po
         product(1, 0, 512, "bank3", "scalar")
         product(1, 512, 512, "bank4", "scalar")
 
-        def gather(got, b, d, cols):
-            entries = places[d][:, cols.start // LANES : cols.stop // LANES]
-            nc.vector.tensor_copy(out=got[:, cols], in_=ys[b][:].indirect(entries))
+        def gather(got, b, d, v0, v1):
+            nc.vector.tensor_copy(out=got, in_=ys[b][:].indirect(places[d][:, v0 // LANES : v1 // LANES]))
 
-        def finish(b, lo, cap, cols, queue):
-            med = keep.tile([P, cols.stop - cols.start], F32, name=f"med{b}_{cols.start}")
-            nc.vector.tensor_tensor(med[:], lo[:, cols], cap[:, cols], MAX)
-            queue.dma_start(out=out[P * b : P * (b + 1), cols], in_=med[:])
+        rest = V - SIDE
+        wide = rest + V
+        side, gaps, signs, parts = ([keep.tile([P, SIDE], F32, name=f"{what}{d}") for d in range(3)] for what in ("side", "gap", "sign", "part"))
+        picked = [gaps[0], gaps[2], gaps[1]]
+        across = keep.tile([P, 3 * SIDE], F32, name="across")
+        near = [keep.tile([P, wide], F32, name=f"near{d}") for d in range(3)]
+        for d in range(3):
+            gather(side[d][:], 0, d, 0, SIDE)
+        for d in range(3):
+            gather(near[d][:, 0:rest], 0, d, SIDE, V)
+        for d in range(3):
+            gather(near[d][:, rest:wide], 1, d, 0, V)
 
-        whole = slice(0, V)
-        n0, n1, n2, hi, lo, cap = ([keep.tile([P, V], F32, name=f"{what}_{b}") for b in range(2)] for what in ("n0", "n1", "n2", "hi", "lo", "cap"))
-        gather(n0[0], 0, 0, whole)
-        gather(n1[0], 0, 1, whole)
-        gather(n2[0], 0, 2, whole)
-        nc.vector.tensor_tensor(hi[0][:], n0[0][:], n1[0][:], MAX)
-        nc.vector.tensor_tensor(lo[0][:], n0[0][:], n1[0][:], MIN)
-        nc.vector.tensor_tensor(cap[0][:], hi[0][:], n2[0][:], MIN)
-        gather(n0[1], 1, 0, whole)
-        finish(0, lo[0], cap[0], whole, nc.sync)
-        gather(n1[1], 1, 1, whole)
-        gather(n2[1], 1, 2, whole)
-        nc.vector.tensor_tensor(hi[1][:], n0[1][:], n1[1][:], MAX)
-        nc.vector.tensor_tensor(lo[1][:], n0[1][:], n1[1][:], MIN)
-        ends = (slice(0, 192), slice(192, 384), slice(384, V))
-        for cols in ends:
-            nc.vector.tensor_tensor(cap[1][:, cols], hi[1][:, cols], n2[1][:, cols], MIN)
-        for cols, queue in zip(ends, (nc.sync, nc.scalar, nc.sync)):
-            finish(1, lo[1], cap[1], cols, queue)
+        blocks = [slice(P * j, P * (j + 1)) for j in range(SIDE // P)]
+
+        def turn(banks, tile, start, stop):
+            for bank, cols in zip(banks, blocks):
+                nc.tensor.matmul(bank, lhsT=tile[:, cols], rhs=identity[:], is_transpose=True, start=start, stop=stop)
+
+        sums = [[psum.tile([P, 512], F32, name=f"sums{d}_{j}", tag=f"bank{2 + 2 * i + j}") for j in range(2)] for i, d in enumerate((1, 2, 0))]
+        sums = {d: [bank[:, 0:P] for bank in pair] for d, pair in zip((1, 2, 0), sums)}
+        values = [psum.tile([P, 512], F32, name=f"values{i}", tag=f"bank{i}") for i in range(2)]
+        for d in range(3):
+            nc.gpsimd.tensor_tensor(gaps[d][:], side[d][:], side[(d + 1) % 3][:], SUB)
+            tie = ties[:, 1:2] if d == 2 else ties[:, 0:1]
+            nc.scalar.activation(signs[d][:], gaps[d][:], SIGN, bias=tie, scale=TIE_SCALE)
+            c0 = SIDE * (d % 2)
+            turn([values[d // 2][:, c0 + cols.start : c0 + cols.stop] for cols in blocks], side[d], True, True)
+        for d in range(3):
+            for e in sorted((d, (d + 1) % 3), key=lambda e: (e - 1) % 3):
+                closes = d == max(e, (e - 1) % 3)
+                turn(sums[e], signs[d], not closes, closes)
+                if closes:
+                    for bank, cols in zip(sums[e], blocks):
+                        nc.scalar.activation(picked[e][:, cols], bank, ABS, scale=0.5)
+            if d < 2:
+                width = SIDE * (2 - d)
+                nc.scalar.copy(out=across[:, 2 * SIDE * d : 2 * SIDE * d + width], in_=values[d][:, 0:width])
+        total = [psum.tile([P, 512], F32, name=f"total{j}", tag=f"bank{j}") for j in range(len(blocks))]
+        for i, d in enumerate((1, 2, 0)):
+            nc.gpsimd.tensor_tensor(parts[d][:], picked[d][:], across[:, SIDE * d : SIDE * (d + 1)], MULT)
+            turn([bank[:, 0:P] for bank in total], parts[d], i == 0, i == 2)
+        side_med = keep.tile([P, SIDE], F32, name="side_med")
+        for j, cols in enumerate(blocks):
+            nc.scalar.copy(out=side_med[:, cols], in_=total[j][:, 0:P])
+        nc.scalar.dma_start(out=out[0:P, 0:SIDE], in_=side_med[:])
+
+        hi, lo, cap, med = (keep.tile([P, wide], F32, name=what) for what in ("hi", "lo", "cap", "med"))
+        nc.vector.tensor_tensor(hi[:], near[0][:], near[1][:], MAX)
+        nc.vector.tensor_tensor(lo[:], near[0][:], near[1][:], MIN)
+        ends = ((0, rest), (rest, rest + 256), (rest + 256, rest + 384), (rest + 384, wide))
+
+        def capped(c0, c1):
+            nc.vector.tensor_tensor(cap[:, c0:c1], hi[:, c0:c1], near[2][:, c0:c1], MIN)
+
+        def finish(c0, c1, queue):
+            nc.vector.tensor_tensor(med[:, c0:c1], lo[:, c0:c1], cap[:, c0:c1], MAX)
+            if c1 <= rest:
+                queue.dma_start(out=out[0:P, SIDE + c0 : SIDE + c1], in_=med[:, c0:c1])
+            else:
+                queue.dma_start(out=out[P : 2 * P, c0 - rest : c1 - rest], in_=med[:, c0:c1])
+
+        capped(*ends[0])
+        capped(*ends[1])
+        finish(*ends[0], nc.sync)
+        capped(ends[2][0], ends[3][1])
+        finish(*ends[1], nc.sync)
+        finish(*ends[2], nc.scalar)
+        finish(*ends[3], nc.sync)

@@ -138,16 +138,19 @@ def tile_picked_median_none_e_kernel(tc, xT, w1_words, w1_scales, offs, pos1, po
 
         rest = V - SIDE
         wide = rest + V
-        side, gaps, signs, parts = ([keep.tile([P, SIDE], F32, name=f"{what}{d}") for d in range(3)] for what in ("side", "gap", "sign", "part"))
-        picked = [gaps[0], gaps[2], gaps[1]]
+        lo, cap, med = (keep.tile([P, wide], F32, name=what) for what in ("lo", "cap", "med"))
+        gaps, signs = ([keep.tile([P, SIDE], F32, name=f"{what}{d}")[:] for d in range(3)] for what in ("gap", "sign"))
+        side = [lo[:, 0:SIDE]] + [keep.tile([P, SIDE], F32, name=f"side{d}")[:] for d in (1, 2)]
+        picked = [lo[:, SIDE : 2 * SIDE], gaps[2], lo[:, 2 * SIDE : 3 * SIDE]]
+        parts = keep.tile([P, 3 * SIDE], F32, name="parts")
         across = keep.tile([P, 3 * SIDE], F32, name="across")
-        near = [keep.tile([P, wide], F32, name=f"near{d}") for d in range(3)]
+        near = [keep.tile([P, V], F32, name=f"near{d}") for d in range(3)]
+        others = [near[0][:, SIDE:V], near[1][:, 0:rest], near[2][:, 0:rest]]
         for d in range(3):
-            gather(side[d][:], 0, d, 0, SIDE)
+            gather(side[d], 0, d, 0, SIDE)
         for d in range(3):
-            gather(near[d][:, 0:rest], 0, d, SIDE, V)
-        for d in range(3):
-            gather(near[d][:, rest:wide], 1, d, 0, V)
+            gather(others[d], 0, d, SIDE, V)
+        gather(near[0][:, 0:SIDE], 1, 0, 0, SIDE)
 
         blocks = [slice(P * j, P * (j + 1)) for j in range(SIDE // P)]
 
@@ -159,11 +162,17 @@ def tile_picked_median_none_e_kernel(tc, xT, w1_words, w1_scales, offs, pos1, po
         sums = {d: [bank[:, 0:P] for bank in pair] for d, pair in zip((1, 2, 0), sums)}
         values = [psum.tile([P, 512], F32, name=f"values{i}", tag=f"bank{i}") for i in range(2)]
         for d in range(3):
-            nc.gpsimd.tensor_tensor(gaps[d][:], side[d][:], side[(d + 1) % 3][:], SUB)
+            nc.gpsimd.tensor_tensor(gaps[d], side[d], side[(d + 1) % 3], SUB)
             tie = ties[:, 1:2] if d == 2 else ties[:, 0:1]
-            nc.scalar.activation(signs[d][:], gaps[d][:], SIGN, bias=tie, scale=TIE_SCALE)
-            c0 = SIDE * (d % 2)
+            nc.scalar.activation(signs[d], gaps[d], SIGN, bias=tie, scale=TIE_SCALE)
+            c0 = SIDE * (d == 0)
             turn([values[d // 2][:, c0 + cols.start : c0 + cols.stop] for cols in blocks], side[d], True, True)
+        nc.vector.tensor_tensor(side[2], others[0], others[1], MAX)
+        nc.vector.tensor_tensor(lo[:, 0:rest], others[0], others[1], MIN)
+        nc.vector.tensor_tensor(cap[:, 0:rest], side[2], others[2], MIN)
+        gather(near[0][:, SIDE:V], 1, 0, SIDE, V)
+        for d in (1, 2):
+            gather(near[d][:], 1, d, 0, V)
         for d in range(3):
             for e in sorted((d, (d + 1) % 3), key=lambda e: (e - 1) % 3):
                 closes = d == max(e, (e - 1) % 3)
@@ -175,33 +184,34 @@ def tile_picked_median_none_e_kernel(tc, xT, w1_words, w1_scales, offs, pos1, po
                 width = SIDE * (2 - d)
                 nc.scalar.copy(out=across[:, 2 * SIDE * d : 2 * SIDE * d + width], in_=values[d][:, 0:width])
         total = [psum.tile([P, 512], F32, name=f"total{j}", tag=f"bank{j}") for j in range(len(blocks))]
-        for i, d in enumerate((1, 2, 0)):
-            nc.gpsimd.tensor_tensor(parts[d][:], picked[d][:], across[:, SIDE * d : SIDE * (d + 1)], MULT)
-            turn([bank[:, 0:P] for bank in total], parts[d], i == 0, i == 2)
+        nc.gpsimd.tensor_tensor(parts[:, 0:SIDE], picked[1], across[:, 0:SIDE], MULT)
+        nc.gpsimd.tensor_tensor(parts[:, SIDE : 3 * SIDE], lo[:, SIDE : 3 * SIDE], across[:, SIDE : 3 * SIDE], MULT)
+        for i in range(3):
+            turn([bank[:, 0:P] for bank in total], parts[:, SIDE * i : SIDE * (i + 1)], i == 0, i == 2)
         side_med = keep.tile([P, SIDE], F32, name="side_med")
         for j, cols in enumerate(blocks):
             nc.scalar.copy(out=side_med[:, cols], in_=total[j][:, 0:P])
         nc.scalar.dma_start(out=out[0:P, 0:SIDE], in_=side_med[:])
 
-        hi, lo, cap, med = (keep.tile([P, wide], F32, name=what) for what in ("hi", "lo", "cap", "med"))
-        nc.vector.tensor_tensor(hi[:], near[0][:], near[1][:], MAX)
-        nc.vector.tensor_tensor(lo[:], near[0][:], near[1][:], MIN)
-        ends = ((0, rest), (rest, rest + 256), (rest + 256, rest + 384), (rest + 384, wide))
+        hi = across[:, 0:V]
+        nc.vector.tensor_tensor(hi, near[0][:], near[1][:], MAX)
+        nc.vector.tensor_tensor(lo[:, rest:wide], near[0][:], near[1][:], MIN)
 
         def capped(c0, c1):
-            nc.vector.tensor_tensor(cap[:, c0:c1], hi[:, c0:c1], near[2][:, c0:c1], MIN)
+            nc.vector.tensor_tensor(cap[:, rest + c0 : rest + c1], hi[:, c0:c1], near[2][:, c0:c1], MIN)
 
-        def finish(c0, c1, queue):
+        def finish(c0, c1):
             nc.vector.tensor_tensor(med[:, c0:c1], lo[:, c0:c1], cap[:, c0:c1], MAX)
-            if c1 <= rest:
-                queue.dma_start(out=out[0:P, SIDE + c0 : SIDE + c1], in_=med[:, c0:c1])
-            else:
-                queue.dma_start(out=out[P : 2 * P, c0 - rest : c1 - rest], in_=med[:, c0:c1])
 
-        capped(*ends[0])
-        capped(*ends[1])
-        finish(*ends[0], nc.sync)
-        capped(ends[2][0], ends[3][1])
-        finish(*ends[1], nc.sync)
-        finish(*ends[2], nc.scalar)
-        finish(*ends[3], nc.sync)
+        def store(c0, c1, queue):
+            queue.dma_start(out=out[P : 2 * P, c0:c1], in_=med[:, rest + c0 : rest + c1])
+
+        capped(0, 128)
+        capped(128, V)
+        finish(0, rest + 128)
+        nc.sync.dma_start(out=out[0:P, SIDE:V], in_=med[:, 0:rest])
+        store(0, 128, nc.scalar)
+        finish(rest + 128, rest + 384)
+        store(128, 384, nc.sync)
+        finish(rest + 384, wide)
+        store(384, V, nc.scalar)

@@ -38,6 +38,7 @@ VECTOR_SHARE = (416, 416, 416, 416)
 LAST_PIECE = 256
 STRETCHES = ((0, 256), (512, 256), (256, 256), (768, 128), (896, 128))
 SIDE = 256
+EARLY = 512
 TIE_SCALE = 2.0**40
 TIE_BIAS = 2.0**-110
 
@@ -71,11 +72,11 @@ def tile_picked_median_none_e_kernel(tc, xT, w1_words, w1_scales, offs, pos1, po
                 if t == LOAD_ORDER[0] and c0 == 0:
                     nc.sync.dma_start(picks[:], offs)
                 c0 = c0 + width
+        for place, pos in zip(places, (pos1, pos2, pos3)):
+            nc.sync.dma_start(place[:], pos)
         nc.sync.dma_start(out=w_words[:], in_=w1_words[0])
         for q in range(4):
             nc.sync.dma_start(out=w_scales[32 * q : 32 * q + 4, :].bitcast(I32), in_=w1_scales[0, 4 * q : 4 * q + 4, :].bitcast(I32))
-        for place, pos in zip(places, (pos1, pos2, pos3)):
-            nc.sync.dma_start(place[:], pos)
 
         quads = keep.tile([P, 4 * S], BF16, name="quads", align_bytes=64)
         slots = quads[:].rearrange("p (n t) -> p n t", t=4)
@@ -145,12 +146,12 @@ def tile_picked_median_none_e_kernel(tc, xT, w1_words, w1_scales, offs, pos1, po
         parts = keep.tile([P, 3 * SIDE], F32, name="parts")
         across = keep.tile([P, 3 * SIDE], F32, name="across")
         near = [keep.tile([P, V], F32, name=f"near{d}") for d in range(3)]
-        others = [near[0][:, SIDE:V], near[1][:, 0:rest], near[2][:, 0:rest]]
+        others = [near[1][:, 0:rest], near[1][:, rest : 2 * rest], near[2][:, 0:rest]]
         for d in range(3):
             gather(side[d], 0, d, 0, SIDE)
         for d in range(3):
             gather(others[d], 0, d, SIDE, V)
-        gather(near[0][:, 0:SIDE], 1, 0, 0, SIDE)
+        gather(near[0][:, 0:EARLY], 1, 0, 0, EARLY)
 
         blocks = [slice(P * j, P * (j + 1)) for j in range(SIDE // P)]
 
@@ -170,7 +171,6 @@ def tile_picked_median_none_e_kernel(tc, xT, w1_words, w1_scales, offs, pos1, po
         nc.vector.tensor_tensor(side[2], others[0], others[1], MAX)
         nc.vector.tensor_tensor(lo[:, 0:rest], others[0], others[1], MIN)
         nc.vector.tensor_tensor(cap[:, 0:rest], side[2], others[2], MIN)
-        gather(near[0][:, SIDE:V], 1, 0, SIDE, V)
         for d in (1, 2):
             gather(near[d][:], 1, d, 0, V)
         for d in range(3):
@@ -193,25 +193,15 @@ def tile_picked_median_none_e_kernel(tc, xT, w1_words, w1_scales, offs, pos1, po
             nc.scalar.copy(out=side_med[:, cols], in_=total[j][:, 0:P])
         nc.scalar.dma_start(out=out[0:P, 0:SIDE], in_=side_med[:])
 
+        rest_med = across[:, V : V + rest]
+        nc.vector.tensor_tensor(rest_med, lo[:, 0:rest], cap[:, 0:rest], MAX)
+        nc.sync.dma_start(out=out[0:P, SIDE:V], in_=rest_med)
         hi = across[:, 0:V]
-        nc.vector.tensor_tensor(hi, near[0][:], near[1][:], MAX)
-        nc.vector.tensor_tensor(lo[:, rest:wide], near[0][:], near[1][:], MIN)
-
-        def capped(c0, c1):
+        nc.vector.tensor_tensor(hi, near[0][:, 0:V], near[1][:], MAX)
+        nc.vector.tensor_tensor(lo[:, rest:wide], near[0][:, 0:V], near[1][:], MIN)
+        ends = ((0, 192), (192, 384), (384, V))
+        for c0, c1 in ends:
             nc.vector.tensor_tensor(cap[:, rest + c0 : rest + c1], hi[:, c0:c1], near[2][:, c0:c1], MIN)
-
-        def finish(c0, c1):
-            nc.vector.tensor_tensor(med[:, c0:c1], lo[:, c0:c1], cap[:, c0:c1], MAX)
-
-        def store(c0, c1, queue):
-            queue.dma_start(out=out[P : 2 * P, c0:c1], in_=med[:, rest + c0 : rest + c1])
-
-        capped(0, 128)
-        capped(128, V)
-        finish(0, rest + 128)
-        nc.sync.dma_start(out=out[0:P, SIDE:V], in_=med[:, 0:rest])
-        store(0, 128, nc.scalar)
-        finish(rest + 128, rest + 384)
-        store(128, 384, nc.sync)
-        finish(rest + 384, wide)
-        store(384, V, nc.scalar)
+        for (c0, c1), queue in zip(ends, (nc.sync, nc.scalar, nc.sync)):
+            nc.vector.tensor_tensor(med[:, c0:c1], lo[:, rest + c0 : rest + c1], cap[:, rest + c0 : rest + c1], MAX)
+            queue.dma_start(out=out[P : 2 * P, c0:c1], in_=med[:, c0:c1])

@@ -16,7 +16,6 @@ FP8X4 = mybir.dt.float8_e4m3fn_x4
 FP4X4 = mybir.dt.float4_e2m1fn_x4
 MAX = mybir.AluOpType.max
 MIN = mybir.AluOpType.min
-ADD = mybir.AluOpType.add
 SUB = mybir.AluOpType.subtract
 MULT = mybir.AluOpType.mult
 COPY = mybir.ActivationFunctionType.Copy
@@ -25,22 +24,29 @@ ABS = mybir.ActivationFunctionType.Abs
 
 P = 128
 LANES = 16
+BANK = 512
+PLANES = 4
+HALF = T // 2
+QUARTER = T // 4
 
-LOAD_ORDER = (2, 0, 1, 3)
-CHUNKS = (
-    ((2048, "both"),),
-    ((1024, "gpsimd"), (1024, "vector")),
-    ((512, "gpsimd"), (512, "gpsimd"), (1024, "vector")),
-    ((512, "gpsimd"), (512, "gpsimd"), (512, "vector"), (512, "vector")),
-)
-FIRST_SPLIT = 1280
-VECTOR_SHARE = (416, 416, 416, 416)
-LAST_PIECE = 256
+LOAD_ORDER = (0, 2, 1, 3)
+
+FIRST_ON_VECTOR = 1280
+VECTOR_SHARE = 416
+SCALAR_TAIL = 256
 STRETCHES = ((0, 256), (512, 256), (256, 256), (768, 128), (896, 128))
-SIDE = 256
-EARLY = 512
+EMPTIED_BY_VECTOR = (1, 2)
+MASKED = 2 * P
+REST = V - MASKED
 TIE_SCALE = 2.0**40
 TIE_BIAS = 2.0**-110
+ENDS = (slice(0, 192), slice(192, 384), slice(384, V))
+
+
+def plane_loads(turn_number):
+    first = [(0, HALF)] if turn_number < PLANES - 2 else [(0, QUARTER), (QUARTER, HALF)]
+    second = [(HALF, T)] if turn_number < PLANES - 1 else [(HALF, HALF + QUARTER), (HALF + QUARTER, T)]
+    return [(c0, c1, "gpsimd") for c0, c1 in first] + [(c0, c1, "vector") for c0, c1 in second]
 
 
 def tile_picked_median_none_e_kernel(tc, xT, w1_words, w1_scales, offs, pos1, pos2, pos3, out):
@@ -49,7 +55,10 @@ def tile_picked_median_none_e_kernel(tc, xT, w1_words, w1_scales, offs, pos1, po
         keep = ctx.enter_context(tc.tile_pool(name="keep", bufs=1))
         psum = ctx.enter_context(tc.psum_pool(name="psum", bufs=1))
 
-        x_rows = xT.rearrange("(p j) t -> p j t", j=4)
+        def bank(number, name):
+            return psum.tile([P, BANK], F32, name=name, tag=f"bank{number}")
+
+        x_rows = xT.rearrange("(p t) n -> p t n", t=PLANES)
         picks = keep.tile([P, S // LANES], U16, name="picks")
         places = [keep.tile([P, V // LANES], U16, name=f"places{d}") for d in range(3)]
         w_words = keep.tile([P, 2 * N], U8, name="w_words", align_bytes=64)
@@ -63,145 +72,145 @@ def tile_picked_median_none_e_kernel(tc, xT, w1_words, w1_scales, offs, pos1, po
         nc.gpsimd.memset(ties[:, 0:1], TIE_BIAS)
         nc.gpsimd.memset(ties[:, 1:2], -TIE_BIAS)
 
-        raws = [keep.tile([P, T], F32, name=f"raw{t}") for t in range(4)]
-        rounded = [keep.tile([P, T], BF16, name=f"rounded{t}") for t in range(4)]
-        for chunks, t in zip(CHUNKS, LOAD_ORDER):
-            c0 = 0
-            for width, engine in chunks:
-                nc.sync.dma_start(out=raws[t][:, c0 : c0 + width], in_=x_rows[:, t, c0 : c0 + width])
-                if t == LOAD_ORDER[0] and c0 == 0:
-                    nc.sync.dma_start(picks[:], offs)
-                c0 = c0 + width
+        raws = [keep.tile([P, T], F32, name=f"raw{t}") for t in range(PLANES)]
+        rounded = [keep.tile([P, T], BF16, name=f"rounded{t}") for t in range(PLANES)]
+        nc.sync.dma_start(out=raws[LOAD_ORDER[0]][:], in_=x_rows[:, LOAD_ORDER[0], :])
+        nc.sync.dma_start(picks[:], offs)
+        for i, t in enumerate(LOAD_ORDER[1:]):
+            for c0, c1, engine in plane_loads(i + 1):
+                nc.sync.dma_start(out=raws[t][:, c0:c1], in_=x_rows[:, t, c0:c1])
         for place, pos in zip(places, (pos1, pos2, pos3)):
             nc.sync.dma_start(place[:], pos)
         nc.sync.dma_start(out=w_words[:], in_=w1_words[0])
         for q in range(4):
             nc.sync.dma_start(out=w_scales[32 * q : 32 * q + 4, :].bitcast(I32), in_=w1_scales[0, 4 * q : 4 * q + 4, :].bitcast(I32))
 
-        quads = keep.tile([P, 4 * S], BF16, name="quads", align_bytes=64)
-        slots = quads[:].rearrange("p (n t) -> p n t", t=4)
+        quads = keep.tile([P, PLANES * S], BF16, name="quads", align_bytes=64)
+        slots = quads[:].rearrange("p (j t) -> p j t", t=PLANES)
+        tail = S - SCALAR_TAIL
+        shared = tail - VECTOR_SHARE
 
-        for chunks, t in zip(CHUNKS, LOAD_ORDER):
-            c0 = 0
-            for width, engine in chunks:
-                cols = slice(c0, c0 + width)
-                if engine == "vector":
-                    nc.vector.tensor_copy(out=rounded[t][:, cols], in_=raws[t][:, cols])
-                elif engine == "both":
-                    nc.vector.tensor_copy(out=rounded[t][:, 0:FIRST_SPLIT], in_=raws[t][:, 0:FIRST_SPLIT])
-                    nc.scalar.copy(out=rounded[t][:, FIRST_SPLIT:T], in_=raws[t][:, FIRST_SPLIT:T])
-                elif engine == "gpsimd":
-                    nc.gpsimd.tensor_copy(out=rounded[t][:, cols], in_=raws[t][:, cols])
-                else:
-                    nc.scalar.copy(out=rounded[t][:, cols], in_=raws[t][:, cols])
-                c0 = c0 + width
-            for e0, count in ((S - LAST_PIECE - VECTOR_SHARE[t], VECTOR_SHARE[t]),):
-                entries = picks[:, e0 // LANES : (e0 + count) // LANES]
-                nc.vector.tensor_copy(out=slots[:, e0 : e0 + count, t], in_=raws[t][:].indirect(entries))
-            for e0, count in ((0, S - LAST_PIECE - VECTOR_SHARE[t]), (S - LAST_PIECE, LAST_PIECE)):
-                entries = picks[:, e0 // LANES : (e0 + count) // LANES]
-                nc.scalar.activation(slots[:, e0 : e0 + count, t], rounded[t][:].indirect(entries), COPY)
+        def entries(e0, e1):
+            return picks[:, e0 // LANES : e1 // LANES]
+
+        for i, t in enumerate(LOAD_ORDER):
+            if i == 0:
+                nc.vector.tensor_copy(out=rounded[t][:, 0:FIRST_ON_VECTOR], in_=raws[t][:, 0:FIRST_ON_VECTOR])
+                nc.scalar.copy(out=rounded[t][:, FIRST_ON_VECTOR:T], in_=raws[t][:, FIRST_ON_VECTOR:T])
+            else:
+                for c0, c1, engine in plane_loads(i):
+                    rounder = nc.gpsimd if engine == "gpsimd" else nc.vector
+                    rounder.tensor_copy(out=rounded[t][:, c0:c1], in_=raws[t][:, c0:c1])
+            nc.vector.tensor_copy(out=slots[:, shared:tail, t], in_=raws[t][:].indirect(entries(shared, tail)))
+            for e0, e1 in ((0, shared), (tail, S)):
+                nc.scalar.activation(slots[:, e0:e1, t], rounded[t][:].indirect(entries(e0, e1)), COPY)
 
         codes = keep.tile([P, S], U32, name="codes", align_bytes=64)
         scales = keep.tile([P, S], U8, name="scales", align_bytes=64)
         ys = [keep.tile([P, S], F32, name=f"y{b}") for b in range(2)]
 
-        def product(b, c0, width, tag, engine):
-            acc = psum.tile([P, 512], F32, name=f"acc{b}_{c0}", tag=tag)
+        def product(b, e0, count, number, on_vector):
+            acc = bank(number, f"acc{b}_{e0}")
             nc.tensor.matmul_mx(
-                out=acc[:, 0:width],
+                out=acc[:, 0:count],
                 lhsT=w_words[:, 2 * P * b : 2 * P * (b + 1)].bitcast(FP4X4),
                 lhsT_scale=w_scales[:, P * b : P * (b + 1)],
-                rhs=codes[:, c0 : c0 + width].bitcast(FP8X4),
-                rhs_scale=scales[:, c0 : c0 + width],
+                rhs=codes[:, e0 : e0 + count].bitcast(FP8X4),
+                rhs_scale=scales[:, e0 : e0 + count],
                 start=True,
                 stop=True,
             )
-            if engine == "vector":
-                nc.vector.tensor_copy(out=ys[b][:, c0 : c0 + width], in_=acc[:, 0:width])
-            else:
-                nc.scalar.copy(out=ys[b][:, c0 : c0 + width], in_=acc[:, 0:width])
+            empty = nc.vector.tensor_copy if on_vector else nc.scalar.copy
+            empty(out=ys[b][:, e0 : e0 + count], in_=acc[:, 0:count])
 
-        for i, (c0, width) in enumerate(STRETCHES):
-            cols = slice(c0, c0 + width)
+        for e0, count in STRETCHES:
             nc.vector.quantize_mx(
-                out=codes[:, cols].bitcast(FP8X4),
-                scales=scales[:, cols],
-                in_=quads[:, 4 * c0 : 4 * (c0 + width)],
+                out=codes[:, e0 : e0 + count].bitcast(FP8X4),
+                scales=scales[:, e0 : e0 + count],
+                in_=quads[:, PLANES * e0 : PLANES * (e0 + count)],
             )
-        for i, (c0, width) in enumerate(STRETCHES):
-            product(0, c0, width, f"bank{i}", "vector" if i in (1, 2) else "scalar")
-        product(1, 0, 512, "bank3", "scalar")
-        product(1, 512, 512, "bank4", "scalar")
+        for i, (e0, count) in enumerate(STRETCHES):
+            product(0, e0, count, i, i in EMPTIED_BY_VECTOR)
+        for i in range(S // BANK):
+            product(1, BANK * i, BANK, len(STRETCHES) - 2 + i, False)
 
         def gather(got, b, d, v0, v1):
             nc.vector.tensor_copy(out=got, in_=ys[b][:].indirect(places[d][:, v0 // LANES : v1 // LANES]))
 
-        rest = V - SIDE
-        wide = rest + V
-        lo, cap, med = (keep.tile([P, wide], F32, name=what) for what in ("lo", "cap", "med"))
-        gaps, signs = ([keep.tile([P, SIDE], F32, name=f"{what}{d}")[:] for d in range(3)] for what in ("gap", "sign"))
-        side = [lo[:, 0:SIDE]] + [keep.tile([P, SIDE], F32, name=f"side{d}")[:] for d in (1, 2)]
-        picked = [lo[:, SIDE : 2 * SIDE], gaps[2], lo[:, 2 * SIDE : 3 * SIDE]]
-        parts = keep.tile([P, 3 * SIDE], F32, name="parts")
-        across = keep.tile([P, 3 * SIDE], F32, name="across")
-        near = [keep.tile([P, V], F32, name=f"near{d}") for d in range(3)]
-        others = [near[1][:, 0:rest], near[1][:, rest : 2 * rest], near[2][:, 0:rest]]
-        for d in range(3):
-            gather(side[d], 0, d, 0, SIDE)
-        for d in range(3):
-            gather(others[d], 0, d, SIDE, V)
-        gather(near[0][:, 0:EARLY], 1, 0, 0, EARLY)
+        def part(tile, i):
+            return tile[:, MASKED * i : MASKED * (i + 1)]
 
-        blocks = [slice(P * j, P * (j + 1)) for j in range(SIDE // P)]
+        low = keep.tile([P, REST + V], F32, name="low")
+        cap = keep.tile([P, REST + V], F32, name="cap")
+        med = keep.tile([P, REST + V], F32, name="med")
+        gaps, signs = ([keep.tile([P, MASKED], F32, name=f"{what}{d}")[:] for d in range(3)] for what in ("gap", "sign"))
+        masked = [part(low, 0)] + [keep.tile([P, MASKED], F32, name=f"masked{d}")[:] for d in (1, 2)]
+        masks_ac = low[:, MASKED : 3 * MASKED]
+        mask = [part(masks_ac, 0), gaps[2], part(masks_ac, 1)]
+        terms = keep.tile([P, 3 * MASKED], F32, name="terms")
+        turned = keep.tile([P, 3 * MASKED], F32, name="turned")
+        near = [keep.tile([P, V], F32, name=f"near{d}")[:] for d in range(3)]
+        others = [near[1][:, 0:REST], near[1][:, REST : 2 * REST], near[2][:, 0:REST]]
 
-        def turn(banks, tile, start, stop):
-            for bank, cols in zip(banks, blocks):
-                nc.tensor.matmul(bank, lhsT=tile[:, cols], rhs=identity[:], is_transpose=True, start=start, stop=stop)
-
-        sums = [[psum.tile([P, 512], F32, name=f"sums{d}_{j}", tag=f"bank{2 + 2 * i + j}") for j in range(2)] for i, d in enumerate((1, 2, 0))]
-        sums = {d: [bank[:, 0:P] for bank in pair] for d, pair in zip((1, 2, 0), sums)}
-        values = [psum.tile([P, 512], F32, name=f"values{i}", tag=f"bank{i}") for i in range(2)]
         for d in range(3):
-            nc.gpsimd.tensor_tensor(gaps[d], side[d], side[(d + 1) % 3], SUB)
+            gather(masked[d], 0, d, 0, MASKED)
+        for d in range(3):
+            gather(others[d], 0, d, MASKED, V)
+        gather(near[0], 1, 0, 0, V)
+
+        blocks = [slice(P * j, P * (j + 1)) for j in range(MASKED // P)]
+
+        def turn(targets, source, start, stop):
+            for target, cols in zip(targets, blocks):
+                nc.tensor.matmul(target, lhsT=source[:, cols], rhs=identity[:], is_transpose=True, start=start, stop=stop)
+
+        order = (1, 2, 0)
+        sums = {e: [bank(2 + len(blocks) * i + j, f"sums{e}_{j}")[:, 0:P] for j in range(len(blocks))] for i, e in enumerate(order)}
+        values = [bank(i, f"values{i}") for i in range(2)]
+        value_at = [part(values[0], 1), part(values[0], 0), part(values[1], 0)]
+        for d in range(3):
+            nc.gpsimd.tensor_tensor(gaps[d], masked[d], masked[(d + 1) % 3], SUB)
             tie = ties[:, 1:2] if d == 2 else ties[:, 0:1]
             nc.scalar.activation(signs[d], gaps[d], SIGN, bias=tie, scale=TIE_SCALE)
-            c0 = SIDE * (d == 0)
-            turn([values[d // 2][:, c0 + cols.start : c0 + cols.stop] for cols in blocks], side[d], True, True)
-        nc.vector.tensor_tensor(side[2], others[0], others[1], MAX)
-        nc.vector.tensor_tensor(lo[:, 0:rest], others[0], others[1], MIN)
-        nc.vector.tensor_tensor(cap[:, 0:rest], side[2], others[2], MIN)
+            turn([value_at[d][:, cols] for cols in blocks], masked[d], True, True)
+
+        rest_high = masked[2]
+        nc.vector.tensor_tensor(rest_high, others[0], others[1], MAX)
+        nc.vector.tensor_tensor(low[:, 0:REST], others[0], others[1], MIN)
+        nc.vector.tensor_tensor(cap[:, 0:REST], rest_high, others[2], MIN)
         for d in (1, 2):
-            gather(near[d][:], 1, d, 0, V)
+            gather(near[d], 1, d, 0, V)
+
         for d in range(3):
-            for e in sorted((d, (d + 1) % 3), key=lambda e: (e - 1) % 3):
+            for e in sorted((d, (d + 1) % 3), key=order.index):
                 closes = d == max(e, (e - 1) % 3)
                 turn(sums[e], signs[d], not closes, closes)
                 if closes:
-                    for bank, cols in zip(sums[e], blocks):
-                        nc.scalar.activation(picked[e][:, cols], bank, ABS, scale=0.5)
-            if d < 2:
-                width = SIDE * (2 - d)
-                nc.scalar.copy(out=across[:, 2 * SIDE * d : 2 * SIDE * d + width], in_=values[d][:, 0:width])
-        total = [psum.tile([P, 512], F32, name=f"total{j}", tag=f"bank{j}") for j in range(len(blocks))]
-        nc.gpsimd.tensor_tensor(parts[:, 0:SIDE], picked[1], across[:, 0:SIDE], MULT)
-        nc.gpsimd.tensor_tensor(parts[:, SIDE : 3 * SIDE], lo[:, SIDE : 3 * SIDE], across[:, SIDE : 3 * SIDE], MULT)
-        for i in range(3):
-            turn([bank[:, 0:P] for bank in total], parts[:, SIDE * i : SIDE * (i + 1)], i == 0, i == 2)
-        side_med = keep.tile([P, SIDE], F32, name="side_med")
-        for j, cols in enumerate(blocks):
-            nc.scalar.copy(out=side_med[:, cols], in_=total[j][:, 0:P])
-        nc.scalar.dma_start(out=out[0:P, 0:SIDE], in_=side_med[:])
+                    for summed, cols in zip(sums[e], blocks):
+                        nc.scalar.activation(mask[e][:, cols], summed, ABS, scale=0.5)
+            if d == 0:
+                nc.scalar.copy(out=turned[:, 0 : 2 * MASKED], in_=values[0][:, 0 : 2 * MASKED])
+            elif d == 1:
+                nc.scalar.copy(out=part(turned, 2), in_=value_at[2])
 
-        rest_med = across[:, V : V + rest]
-        nc.vector.tensor_tensor(rest_med, lo[:, 0:rest], cap[:, 0:rest], MAX)
-        nc.sync.dma_start(out=out[0:P, SIDE:V], in_=rest_med)
-        hi = across[:, 0:V]
-        nc.vector.tensor_tensor(hi, near[0][:, 0:V], near[1][:], MAX)
-        nc.vector.tensor_tensor(lo[:, rest:wide], near[0][:, 0:V], near[1][:], MIN)
-        ends = ((0, 192), (192, 384), (384, V))
-        for c0, c1 in ends:
-            nc.vector.tensor_tensor(cap[:, rest + c0 : rest + c1], hi[:, c0:c1], near[2][:, c0:c1], MIN)
-        for (c0, c1), queue in zip(ends, (nc.sync, nc.scalar, nc.sync)):
-            nc.vector.tensor_tensor(med[:, c0:c1], lo[:, rest + c0 : rest + c1], cap[:, rest + c0 : rest + c1], MAX)
-            queue.dma_start(out=out[P : 2 * P, c0:c1], in_=med[:, c0:c1])
+        total = [bank(j, f"total{j}")[:, 0:P] for j in range(len(blocks))]
+        nc.gpsimd.tensor_tensor(part(terms, 0), mask[1], part(turned, 0), MULT)
+        nc.gpsimd.tensor_tensor(terms[:, MASKED : 3 * MASKED], masks_ac, turned[:, MASKED : 3 * MASKED], MULT)
+        for i in range(3):
+            turn(total, part(terms, i), i == 0, i == 2)
+        masked_med = keep.tile([P, MASKED], F32, name="masked_med")
+        for summed, cols in zip(total, blocks):
+            nc.scalar.copy(out=masked_med[:, cols], in_=summed)
+        nc.scalar.dma_start(out=out[0:P, 0:MASKED], in_=masked_med[:])
+
+        rest_med = turned[:, V : V + REST]
+        nc.vector.tensor_tensor(rest_med, low[:, 0:REST], cap[:, 0:REST], MAX)
+        nc.sync.dma_start(out=out[0:P, MASKED:V], in_=rest_med)
+        last_high, last_low, last_cap = turned[:, 0:V], low[:, REST : REST + V], cap[:, REST : REST + V]
+        nc.vector.tensor_tensor(last_high, near[0], near[1], MAX)
+        nc.vector.tensor_tensor(last_low, near[0], near[1], MIN)
+        for cols in ENDS:
+            nc.vector.tensor_tensor(last_cap[:, cols], last_high[:, cols], near[2][:, cols], MIN)
+        for cols, queue in zip(ENDS, (nc.sync, nc.scalar, nc.sync)):
+            nc.vector.tensor_tensor(med[:, cols], last_low[:, cols], last_cap[:, cols], MAX)
+            queue.dma_start(out=out[P : 2 * P, cols], in_=med[:, cols])

@@ -32,9 +32,10 @@ QUARTER = T // 4
 LOAD_ORDER = (0, 2, 1, 3)
 
 FIRST_ON_VECTOR = 1280
+ON_GPSIMD = 768
 VECTOR_SHARE = 416
 SCALAR_TAIL = 256
-STRETCHES = ((0, 256), (512, 256), (256, 256), (768, 128), (896, 128))
+STRETCHES = ((512, 256), (0, 256), (256, 256), (768, 128), (896, 128))
 EMPTIED_BY_VECTOR = (1, 2)
 MASKED = 2 * P
 REST = V - MASKED
@@ -44,8 +45,8 @@ ENDS = (slice(0, 192), slice(192, 384), slice(384, V))
 
 
 def plane_loads(turn_number):
-    first = [(0, HALF)] if turn_number < PLANES - 2 else [(0, QUARTER), (QUARTER, HALF)]
-    second = [(HALF, T)] if turn_number < PLANES - 1 else [(HALF, HALF + QUARTER), (HALF + QUARTER, T)]
+    first = [(0, ON_GPSIMD)]
+    second = [(ON_GPSIMD, T)] if turn_number < PLANES - 1 else [(ON_GPSIMD, T - QUARTER), (T - QUARTER, T)]
     return [(c0, c1, "gpsimd") for c0, c1 in first] + [(c0, c1, "vector") for c0, c1 in second]
 
 
@@ -88,7 +89,6 @@ def tile_picked_median_none_e_kernel(tc, xT, w1_words, w1_scales, offs, pos1, po
         quads = keep.tile([P, PLANES * S], BF16, name="quads", align_bytes=64)
         slots = quads[:].rearrange("p (j t) -> p j t", t=PLANES)
         tail = S - SCALAR_TAIL
-        shared = tail - VECTOR_SHARE
 
         def entries(e0, e1):
             return picks[:, e0 // LANES : e1 // LANES]
@@ -101,8 +101,9 @@ def tile_picked_median_none_e_kernel(tc, xT, w1_words, w1_scales, offs, pos1, po
                 for c0, c1, engine in plane_loads(i):
                     rounder = nc.gpsimd if engine == "gpsimd" else nc.vector
                     rounder.tensor_copy(out=rounded[t][:, c0:c1], in_=raws[t][:, c0:c1])
-            nc.vector.tensor_copy(out=slots[:, shared:tail, t], in_=raws[t][:].indirect(entries(shared, tail)))
-            for e0, e1 in ((0, shared), (tail, S)):
+            nc.vector.tensor_copy(out=slots[:, 0:VECTOR_SHARE, t], in_=raws[t][:].indirect(entries(0, VECTOR_SHARE)))
+            cuts = (VECTOR_SHARE, S) if i < PLANES - 1 else (VECTOR_SHARE, tail, S)
+            for e0, e1 in zip(cuts, cuts[1:]):
                 nc.scalar.activation(slots[:, e0:e1, t], rounded[t][:].indirect(entries(e0, e1)), COPY)
 
         codes = keep.tile([P, S], U32, name="codes", align_bytes=64)

@@ -46,7 +46,7 @@ ENDS = (slice(0, 192), slice(192, 384), slice(384, V))
 
 def plane_loads(turn_number):
     first = [(0, ON_GPSIMD)]
-    second = [(ON_GPSIMD, T)] if turn_number < PLANES - 1 else [(ON_GPSIMD, T - QUARTER), (T - QUARTER, T)]
+    second = [(ON_GPSIMD, T)] if turn_number < PLANES - 2 else [(ON_GPSIMD, T - QUARTER), (T - QUARTER, T)]
     return [(c0, c1, "gpsimd") for c0, c1 in first] + [(c0, c1, "vector") for c0, c1 in second]
 
 

@@ -1,7 +1,6 @@
 from contextlib import ExitStack
 
 import concourse.mybir as mybir
-from concourse.masks import make_identity
 
 K, T, S, V, N = 512, 2048, 1024, 512, 256
 FLOPS = 2 * K * S * N
@@ -16,11 +15,7 @@ FP8X4 = mybir.dt.float8_e4m3fn_x4
 FP4X4 = mybir.dt.float4_e2m1fn_x4
 MAX = mybir.AluOpType.max
 MIN = mybir.AluOpType.min
-SUB = mybir.AluOpType.subtract
-MULT = mybir.AluOpType.mult
 COPY = mybir.ActivationFunctionType.Copy
-SIGN = mybir.ActivationFunctionType.Sign
-ABS = mybir.ActivationFunctionType.Abs
 
 P = 128
 LANES = 16
@@ -37,11 +32,6 @@ VECTOR_SHARE = 416
 SCALAR_TAIL = 256
 STRETCHES = ((512, 256), (0, 256), (256, 256), (768, 128), (896, 128))
 EMPTIED_BY_VECTOR = (1, 2)
-MASKED = 2 * P
-REST = V - MASKED
-TIE_SCALE = 2.0**40
-TIE_BIAS = 2.0**-110
-ENDS = (slice(0, 192), slice(192, 384), slice(384, V))
 
 
 def plane_loads(turn_number):
@@ -66,12 +56,6 @@ def tile_picked_median_none_e_kernel(tc, xT, w1_words, w1_scales, offs, pos1, po
         w_scales = keep.tile([P, N], U8, name="w_scales", align_bytes=64)
 
         nc.vector.memset(w_scales[:].bitcast(I32), 0)
-
-        identity = keep.tile([P, P], F32, name="identity")
-        make_identity(nc, identity[:])
-        ties = keep.tile([P, 2], F32, name="ties")
-        nc.gpsimd.memset(ties[:, 0:1], TIE_BIAS)
-        nc.gpsimd.memset(ties[:, 1:2], -TIE_BIAS)
 
         raws = [keep.tile([P, T], F32, name=f"raw{t}") for t in range(PLANES)]
         rounded = [keep.tile([P, T], BF16, name=f"rounded{t}") for t in range(PLANES)]
@@ -135,83 +119,39 @@ def tile_picked_median_none_e_kernel(tc, xT, w1_words, w1_scales, offs, pos1, po
         for i in range(S // BANK):
             product(1, BANK * i, BANK, len(STRETCHES) - 2 + i, False)
 
-        def gather(got, b, d, v0, v1):
-            nc.vector.tensor_copy(out=got, in_=ys[b][:].indirect(places[d][:, v0 // LANES : v1 // LANES]))
+        near = [[keep.tile([P, V], F32, name=f"near{b}_{d}") for d in range(3)] for b in range(2)]
+        high, low, cap, med = ([keep.tile([P, V], F32, name=f"{what}{b}") for b in range(2)] for what in ("high", "low", "cap", "med"))
 
-        def part(tile, i):
-            return tile[:, MASKED * i : MASKED * (i + 1)]
+        def gather(on_vector, b, d, v0, v1):
+            window = ys[b][:].indirect(places[d][:, v0 // LANES : v1 // LANES])
+            if on_vector:
+                nc.vector.tensor_copy(out=near[b][d][:, v0:v1], in_=window)
+            else:
+                nc.scalar.activation(near[b][d][:, v0:v1], window, COPY)
 
-        low = keep.tile([P, REST + V], F32, name="low")
-        cap = keep.tile([P, REST + V], F32, name="cap")
-        med = keep.tile([P, REST + V], F32, name="med")
-        gaps, signs = ([keep.tile([P, MASKED], F32, name=f"{what}{d}")[:] for d in range(3)] for what in ("gap", "sign"))
-        masked = [part(low, 0)] + [keep.tile([P, MASKED], F32, name=f"masked{d}")[:] for d in (1, 2)]
-        masks_ac = low[:, MASKED : 3 * MASKED]
-        mask = [part(masks_ac, 0), gaps[2], part(masks_ac, 1)]
-        terms = keep.tile([P, 3 * MASKED], F32, name="terms")
-        turned = keep.tile([P, 3 * MASKED], F32, name="turned")
-        near = [keep.tile([P, V], F32, name=f"near{d}")[:] for d in range(3)]
-        others = [near[1][:, 0:REST], near[1][:, REST : 2 * REST], near[2][:, 0:REST]]
+        def pair(b, v0, v1):
+            nc.vector.tensor_tensor(high[b][:, v0:v1], near[b][0][:, v0:v1], near[b][1][:, v0:v1], MAX)
+            nc.vector.tensor_tensor(low[b][:, v0:v1], near[b][0][:, v0:v1], near[b][1][:, v0:v1], MIN)
 
+        def finish(b, cuts, queues):
+            pieces = [slice(v0, v1) for v0, v1 in zip(cuts, cuts[1:])]
+            for cols in pieces:
+                nc.vector.tensor_tensor(cap[b][:, cols], high[b][:, cols], near[b][2][:, cols], MIN)
+            for cols, queue in zip(pieces, queues):
+                nc.vector.tensor_tensor(med[b][:, cols], low[b][:, cols], cap[b][:, cols], MAX)
+                queue.dma_start(out=out[P * b : P * (b + 1), cols], in_=med[b][:, cols])
+
+        gather(True, 0, 0, 0, V)
+        gather(True, 0, 1, 0, 256)
+        gather(False, 0, 1, 256, V)
+        gather(False, 0, 2, 0, V)
+        pair(0, 0, V)
+        finish(0, (0, 256, V), (nc.sync, nc.sync))
         for d in range(3):
-            gather(masked[d], 0, d, 0, MASKED)
+            gather(False, 1, d, 0, 256)
+        pair(1, 0, 256)
+        finish(1, (0, 128, 256), (nc.sync, nc.sync))
         for d in range(3):
-            gather(others[d], 0, d, MASKED, V)
-        gather(near[0], 1, 0, 0, V)
-
-        blocks = [slice(P * j, P * (j + 1)) for j in range(MASKED // P)]
-
-        def turn(targets, source, start, stop):
-            for target, cols in zip(targets, blocks):
-                nc.tensor.matmul(target, lhsT=source[:, cols], rhs=identity[:], is_transpose=True, start=start, stop=stop)
-
-        order = (1, 2, 0)
-        sums = {e: [bank(2 + len(blocks) * i + j, f"sums{e}_{j}")[:, 0:P] for j in range(len(blocks))] for i, e in enumerate(order)}
-        values = [bank(i, f"values{i}") for i in range(2)]
-        value_at = [part(values[0], 1), part(values[0], 0), part(values[1], 0)]
-        for d in range(3):
-            nc.gpsimd.tensor_tensor(gaps[d], masked[d], masked[(d + 1) % 3], SUB)
-            tie = ties[:, 1:2] if d == 2 else ties[:, 0:1]
-            nc.scalar.activation(signs[d], gaps[d], SIGN, bias=tie, scale=TIE_SCALE)
-            turn([value_at[d][:, cols] for cols in blocks], masked[d], True, True)
-
-        rest_high = masked[2]
-        nc.vector.tensor_tensor(rest_high, others[0], others[1], MAX)
-        nc.vector.tensor_tensor(low[:, 0:REST], others[0], others[1], MIN)
-        nc.vector.tensor_tensor(cap[:, 0:REST], rest_high, others[2], MIN)
-        for d in (1, 2):
-            gather(near[d], 1, d, 0, V)
-
-        for d in range(3):
-            for e in sorted((d, (d + 1) % 3), key=order.index):
-                closes = d == max(e, (e - 1) % 3)
-                turn(sums[e], signs[d], not closes, closes)
-                if closes:
-                    for summed, cols in zip(sums[e], blocks):
-                        nc.scalar.activation(mask[e][:, cols], summed, ABS, scale=0.5)
-            if d == 0:
-                nc.scalar.copy(out=turned[:, 0 : 2 * MASKED], in_=values[0][:, 0 : 2 * MASKED])
-            elif d == 1:
-                nc.scalar.copy(out=part(turned, 2), in_=value_at[2])
-
-        total = [bank(j, f"total{j}")[:, 0:P] for j in range(len(blocks))]
-        nc.gpsimd.tensor_tensor(part(terms, 0), mask[1], part(turned, 0), MULT)
-        nc.gpsimd.tensor_tensor(terms[:, MASKED : 3 * MASKED], masks_ac, turned[:, MASKED : 3 * MASKED], MULT)
-        for i in range(3):
-            turn(total, part(terms, i), i == 0, i == 2)
-        masked_med = keep.tile([P, MASKED], F32, name="masked_med")
-        for summed, cols in zip(total, blocks):
-            nc.scalar.copy(out=masked_med[:, cols], in_=summed)
-        nc.scalar.dma_start(out=out[0:P, 0:MASKED], in_=masked_med[:])
-
-        rest_med = turned[:, V : V + REST]
-        nc.vector.tensor_tensor(rest_med, low[:, 0:REST], cap[:, 0:REST], MAX)
-        nc.sync.dma_start(out=out[0:P, MASKED:V], in_=rest_med)
-        last_high, last_low, last_cap = turned[:, 0:V], low[:, REST : REST + V], cap[:, REST : REST + V]
-        nc.vector.tensor_tensor(last_high, near[0], near[1], MAX)
-        nc.vector.tensor_tensor(last_low, near[0], near[1], MIN)
-        for cols in ENDS:
-            nc.vector.tensor_tensor(last_cap[:, cols], last_high[:, cols], near[2][:, cols], MIN)
-        for cols, queue in zip(ENDS, (nc.sync, nc.scalar, nc.sync)):
-            nc.vector.tensor_tensor(med[:, cols], last_low[:, cols], last_cap[:, cols], MAX)
-            queue.dma_start(out=out[P : 2 * P, cols], in_=med[:, cols])
+            gather(False, 1, d, 256, V)
+        pair(1, 256, V)
+        finish(1, (256, 384, V), (nc.sync, nc.scalar))

@@ -21,23 +21,11 @@ P = 128
 LANES = 16
 BANK = 512
 PLANES = 4
-HALF = T // 2
-QUARTER = T // 4
 
-LOAD_ORDER = (0, 2, 1, 3)
-
-FIRST_ON_VECTOR = 1280
-ON_GPSIMD = 768
-VECTOR_SHARE = 416
-SCALAR_TAIL = 256
-STRETCHES = ((512, 256), (0, 256), (256, 256), (768, 128), (896, 128))
-EMPTIED_BY_VECTOR = (1, 2)
-
-
-def plane_loads(turn_number):
-    first = [(0, ON_GPSIMD)]
-    second = [(ON_GPSIMD, T)] if turn_number < PLANES - 2 else [(ON_GPSIMD, T - QUARTER), (T - QUARTER, T)]
-    return [(c0, c1, "gpsimd") for c0, c1 in first] + [(c0, c1, "vector") for c0, c1 in second]
+EARLY_ON_VECTOR = (896, 256)
+PIECES = ((256, 512), (512, 768), (768, 896), (896, 1024))
+DIRECT = 256
+STRETCHES = ((0, 256), (256, 512), (512, 768), (768, 896), (896, 1024))
 
 
 def tile_picked_median_none_e_kernel(tc, xT, w1_words, w1_scales, offs, pos1, pos2, pos3, out):
@@ -45,9 +33,6 @@ def tile_picked_median_none_e_kernel(tc, xT, w1_words, w1_scales, offs, pos1, po
     with ExitStack() as ctx:
         keep = ctx.enter_context(tc.tile_pool(name="keep", bufs=1))
         psum = ctx.enter_context(tc.psum_pool(name="psum", bufs=1))
-
-        def bank(number, name):
-            return psum.tile([P, BANK], F32, name=name, tag=f"bank{number}")
 
         x_rows = xT.rearrange("(p t) n -> p t n", t=PLANES)
         picks = keep.tile([P, S // LANES], U16, name="picks")
@@ -58,100 +43,128 @@ def tile_picked_median_none_e_kernel(tc, xT, w1_words, w1_scales, offs, pos1, po
         nc.vector.memset(w_scales[:].bitcast(I32), 0)
 
         raws = [keep.tile([P, T], F32, name=f"raw{t}") for t in range(PLANES)]
-        rounded = [keep.tile([P, T], BF16, name=f"rounded{t}") for t in range(PLANES)]
-        nc.sync.dma_start(out=raws[LOAD_ORDER[0]][:], in_=x_rows[:, LOAD_ORDER[0], :])
+        nc.sync.dma_start(out=raws[0][:], in_=x_rows[:, 0, :])
         nc.sync.dma_start(picks[:], offs)
-        for i, t in enumerate(LOAD_ORDER[1:]):
-            for c0, c1, engine in plane_loads(i + 1):
-                nc.sync.dma_start(out=raws[t][:, c0:c1], in_=x_rows[:, t, c0:c1])
-        for place, pos in zip(places, (pos1, pos2, pos3)):
-            nc.sync.dma_start(place[:], pos)
+        for t in range(1, PLANES):
+            nc.sync.dma_start(out=raws[t][:], in_=x_rows[:, t, :])
         nc.sync.dma_start(out=w_words[:], in_=w1_words[0])
         for q in range(4):
             nc.sync.dma_start(out=w_scales[32 * q : 32 * q + 4, :].bitcast(I32), in_=w1_scales[0, 4 * q : 4 * q + 4, :].bitcast(I32))
+        for place, pos in zip(places, (pos1, pos2, pos3)):
+            nc.sync.dma_start(place[:], pos)
 
-        quads = keep.tile([P, PLANES * S], BF16, name="quads", align_bytes=64)
-        slots = quads[:].rearrange("p (j t) -> p j t", t=PLANES)
-        tail = S - SCALAR_TAIL
+        def gather(on_vector, got, window, offsets):
+            if on_vector:
+                nc.vector.tensor_copy(out=got, in_=window[:].indirect(offsets))
+            else:
+                nc.scalar.activation(got, window[:].indirect(offsets), COPY)
 
         def entries(e0, e1):
             return picks[:, e0 // LANES : e1 // LANES]
 
-        for i, t in enumerate(LOAD_ORDER):
-            if i == 0:
-                nc.vector.tensor_copy(out=rounded[t][:, 0:FIRST_ON_VECTOR], in_=raws[t][:, 0:FIRST_ON_VECTOR])
-                nc.scalar.copy(out=rounded[t][:, FIRST_ON_VECTOR:T], in_=raws[t][:, FIRST_ON_VECTOR:T])
-            else:
-                for c0, c1, engine in plane_loads(i):
-                    rounder = nc.gpsimd if engine == "gpsimd" else nc.vector
-                    rounder.tensor_copy(out=rounded[t][:, c0:c1], in_=raws[t][:, c0:c1])
-            nc.vector.tensor_copy(out=slots[:, 0:VECTOR_SHARE, t], in_=raws[t][:].indirect(entries(0, VECTOR_SHARE)))
-            cuts = (VECTOR_SHARE, S) if i < PLANES - 1 else (VECTOR_SHARE, tail, S)
-            for e0, e1 in zip(cuts, cuts[1:]):
-                nc.scalar.activation(slots[:, e0:e1, t], rounded[t][:].indirect(entries(e0, e1)), COPY)
+        quads = keep.tile([P, PLANES * S], BF16, name="quads", align_bytes=64)
+        halves = quads[:].rearrange("p (j u t) -> p j u t", u=2, t=2)
+
+        def lay(u, e0, e1, pair, on_vector=True):
+            copy = nc.vector.tensor_copy if on_vector else nc.scalar.copy
+            copy(out=halves[:, e0:e1, u, :], in_=pair.rearrange("p t j -> p j t"))
+
+        early = keep.tile([P, 2, S], BF16, name="early")
+        for t, share in enumerate(EARLY_ON_VECTOR):
+            gather(True, early[:, t, 0:share], raws[t], entries(0, share))
+            gather(False, early[:, t, share:S], raws[t], entries(share, S))
+        lay(0, 0, S, early[:])
+        slots = quads[:].rearrange("p (j t) -> p j t", t=PLANES)
+        late = [keep.tile([P, 2, e1 - e0], BF16, name=f"late{e0}") for e0, e1 in PIECES]
+        for t in range(2):
+            nc.vector.tensor_copy(out=slots[:, 0:DIRECT, 2 + t], in_=raws[2 + t][:].indirect(entries(0, DIRECT)))
+            for i, (e0, e1) in enumerate(PIECES):
+                gather(False, late[i][:, t, :], raws[2 + t], entries(e0, e1))
 
         codes = keep.tile([P, S], U32, name="codes", align_bytes=64)
         scales = keep.tile([P, S], U8, name="scales", align_bytes=64)
         ys = [keep.tile([P, S], F32, name=f"y{b}") for b in range(2)]
 
-        def product(b, e0, count, number, on_vector):
-            acc = bank(number, f"acc{b}_{e0}")
+        def quantise(e0, e1):
+            nc.vector.quantize_mx(
+                out=codes[:, e0:e1].bitcast(FP8X4),
+                scales=scales[:, e0:e1],
+                in_=quads[:, PLANES * e0 : PLANES * e1],
+            )
+
+        def product(b, e0, e1, acc):
             nc.tensor.matmul_mx(
-                out=acc[:, 0:count],
+                out=acc,
                 lhsT=w_words[:, 2 * P * b : 2 * P * (b + 1)].bitcast(FP4X4),
                 lhsT_scale=w_scales[:, P * b : P * (b + 1)],
-                rhs=codes[:, e0 : e0 + count].bitcast(FP8X4),
-                rhs_scale=scales[:, e0 : e0 + count],
+                rhs=codes[:, e0:e1].bitcast(FP8X4),
+                rhs_scale=scales[:, e0:e1],
                 start=True,
                 stop=True,
             )
-            empty = nc.vector.tensor_copy if on_vector else nc.scalar.copy
-            empty(out=ys[b][:, e0 : e0 + count], in_=acc[:, 0:count])
 
-        for e0, count in STRETCHES:
-            nc.vector.quantize_mx(
-                out=codes[:, e0 : e0 + count].bitcast(FP8X4),
-                scales=scales[:, e0 : e0 + count],
-                in_=quads[:, PLANES * e0 : PLANES * (e0 + count)],
-            )
-        for i, (e0, count) in enumerate(STRETCHES):
-            product(0, e0, count, i, i in EMPTIED_BY_VECTOR)
-        for i in range(S // BANK):
-            product(1, BANK * i, BANK, len(STRETCHES) - 2 + i, False)
+        def empty(on_vector, b, e0, e1, acc):
+            copy = nc.vector.tensor_copy if on_vector else nc.scalar.copy
+            copy(out=ys[b][:, e0:e1], in_=acc)
 
-        near = [[keep.tile([P, V], F32, name=f"near{b}_{d}") for d in range(3)] for b in range(2)]
-        high, low, cap, med = ([keep.tile([P, V], F32, name=f"{what}{b}") for b in range(2)] for what in ("high", "low", "cap", "med"))
+        lay(1, 256, 512, late[0][:])
+        quantise(0, 256)
+        lay(1, 512, 768, late[1][:])
+        lay(1, 768, 896, late[2][:], False)
+        lay(1, 896, 1024, late[3][:], False)
+        for e0, e1 in STRETCHES[1:]:
+            quantise(e0, e1)
+        lower = [psum.tile([P, BANK], F32, name=f"lower{b}") for b in range(2)]
+        for e0, e1 in STRETCHES[:2]:
+            for b in range(2):
+                product(b, e0, e1, lower[b][:, e0:e1])
+        empty(False, 0, 0, BANK, lower[0][:])
+        for i, (e0, e1) in enumerate(STRETCHES[2:]):
+            acc = psum.tile([P, BANK], F32, name=f"upper0_{i}")[:, 0 : e1 - e0]
+            product(0, e0, e1, acc)
+            empty(i < 2, 0, e0, e1, acc)
+        empty(False, 1, 0, BANK, lower[1][:])
+        upper = psum.tile([P, BANK], F32, name="upper1")
+        product(1, BANK, S, upper[:])
+        empty(False, 1, BANK, S, upper[:])
 
-        def gather(on_vector, b, d, v0, v1):
-            window = ys[b][:].indirect(places[d][:, v0 // LANES : v1 // LANES])
-            if on_vector:
-                nc.vector.tensor_copy(out=near[b][d][:, v0:v1], in_=window)
-            else:
-                nc.scalar.activation(near[b][d][:, v0:v1], window, COPY)
+        near = [keep.tile([P, 2 * V], F32, name=f"near{d}") for d in range(3)]
+        high, low, cap, med = (keep.tile([P, 2 * V], F32, name=what) for what in ("high", "low", "cap", "med"))
 
-        def pair(b, v0, v1):
-            nc.vector.tensor_tensor(high[b][:, v0:v1], near[b][0][:, v0:v1], near[b][1][:, v0:v1], MAX)
-            nc.vector.tensor_tensor(low[b][:, v0:v1], near[b][0][:, v0:v1], near[b][1][:, v0:v1], MIN)
+        def fetch(on_vector, d, c0, c1):
+            b, v0 = divmod(c0, V)
+            gather(on_vector, near[d][:, c0:c1], ys[b], places[d][:, v0 // LANES : (v0 + c1 - c0) // LANES])
 
-        def finish(b, cuts, queues):
-            pieces = [slice(v0, v1) for v0, v1 in zip(cuts, cuts[1:])]
-            for cols in pieces:
-                nc.vector.tensor_tensor(cap[b][:, cols], high[b][:, cols], near[b][2][:, cols], MIN)
-            for cols, queue in zip(pieces, queues):
-                nc.vector.tensor_tensor(med[b][:, cols], low[b][:, cols], cap[b][:, cols], MAX)
-                queue.dma_start(out=out[P * b : P * (b + 1), cols], in_=med[b][:, cols])
+        def step(result, left, right, op, c0, c1):
+            nc.vector.tensor_tensor(result[:, c0:c1], left[:, c0:c1], right[:, c0:c1], op)
 
-        gather(True, 0, 0, 0, V)
-        gather(True, 0, 1, 0, 256)
-        gather(False, 0, 1, 256, V)
-        gather(False, 0, 2, 0, V)
-        pair(0, 0, V)
-        finish(0, (0, 256, V), (nc.sync, nc.sync))
+        def finish(c0, c1, queue):
+            step(med, low, cap, MAX, c0, c1)
+            b, v0 = divmod(c0, V)
+            queue.dma_start(out=out[P * b : P * (b + 1), v0 : v0 + c1 - c0], in_=med[:, c0:c1])
+
+        fetch(True, 0, 0, 512)
+        fetch(True, 1, 256, 512)
+        fetch(False, 1, 0, 256)
+        fetch(False, 2, 0, 512)
         for d in range(3):
-            gather(False, 1, d, 0, 256)
-        pair(1, 0, 256)
-        finish(1, (0, 128, 256), (nc.sync, nc.sync))
-        for d in range(3):
-            gather(False, 1, d, 256, V)
-        pair(1, 256, V)
-        finish(1, (256, 384, V), (nc.sync, nc.scalar))
+            fetch(False, d, 512, 768)
+        for d in range(2):
+            fetch(False, d, 768, 1024)
+        fetch(False, 2, 768, 896)
+        fetch(False, 2, 896, 1024)
+        step(high, near[0], near[1], MAX, 0, 512)
+        step(low, near[0], near[1], MIN, 0, 512)
+        step(cap, high, near[2], MIN, 0, 512)
+        step(high, near[0], near[1], MAX, 512, 768)
+        finish(0, 256, nc.sync)
+        step(low, near[0], near[1], MIN, 512, 768)
+        step(cap, high, near[2], MIN, 512, 768)
+        finish(256, 512, nc.sync)
+        finish(512, 768, nc.sync)
+        step(high, near[0], near[1], MAX, 768, 1024)
+        step(low, near[0], near[1], MIN, 768, 1024)
+        step(cap, high, near[2], MIN, 768, 896)
+        step(cap, high, near[2], MIN, 896, 1024)
+        finish(768, 896, nc.sync)
+        finish(896, 1024, nc.scalar)

@@ -119,13 +119,15 @@ def tile_picked_median_none_e_kernel(tc, xT, w1_words, w1_scales, offs, pos1, po
             for b in range(2):
                 product(b, e0, e1, lower[b][:, e0:e1])
         empty(False, 0, 0, BANK, lower[0][:])
+        upper = psum.tile([P, BANK], F32, name="upper1")
         for i, (e0, e1) in enumerate(STRETCHES[2:]):
             acc = psum.tile([P, BANK], F32, name=f"upper0_{i}")[:, 0 : e1 - e0]
             product(0, e0, e1, acc)
             empty(i < 2, 0, e0, e1, acc)
+            if i == 0:
+                product(1, e0, e1, upper[:, 0:256])
         empty(False, 1, 0, BANK, lower[1][:])
-        upper = psum.tile([P, BANK], F32, name="upper1")
-        product(1, BANK, S, upper[:])
+        product(1, 768, S, upper[:, 256:BANK])
         empty(False, 1, BANK, S, upper[:])
 
         near = [keep.tile([P, 2 * V], F32, name=f"near{d}") for d in range(3)]
@@ -144,27 +146,20 @@ def tile_picked_median_none_e_kernel(tc, xT, w1_words, w1_scales, offs, pos1, po
             queue.dma_start(out=out[P * b : P * (b + 1), v0 : v0 + c1 - c0], in_=med[:, c0:c1])
 
         fetch(True, 0, 0, 512)
-        fetch(True, 1, 256, 512)
-        fetch(False, 1, 0, 256)
+        fetch(True, 0, 512, 896)
+        fetch(False, 1, 0, 512)
+        fetch(False, 0, 896, 1024)
+        fetch(False, 1, 512, 1024)
         fetch(False, 2, 0, 512)
-        for d in range(3):
-            fetch(False, d, 512, 768)
-        for d in range(2):
-            fetch(False, d, 768, 1024)
-        fetch(False, 2, 768, 896)
-        fetch(False, 2, 896, 1024)
-        step(high, near[0], near[1], MAX, 0, 512)
-        step(low, near[0], near[1], MIN, 0, 512)
+        fetch(False, 2, 512, 768)
+        fetch(False, 2, 768, 1024)
+        for c0 in (0, 512):
+            step(high, near[0], near[1], MAX, c0, c0 + 512)
+            step(low, near[0], near[1], MIN, c0, c0 + 512)
         step(cap, high, near[2], MIN, 0, 512)
-        step(high, near[0], near[1], MAX, 512, 768)
-        finish(0, 256, nc.sync)
-        step(low, near[0], near[1], MIN, 512, 768)
         step(cap, high, near[2], MIN, 512, 768)
-        finish(256, 512, nc.sync)
+        finish(0, 512, nc.sync)
+        step(cap, high, near[2], MIN, 768, 1024)
         finish(512, 768, nc.sync)
-        step(high, near[0], near[1], MAX, 768, 1024)
-        step(low, near[0], near[1], MIN, 768, 1024)
-        step(cap, high, near[2], MIN, 768, 896)
-        step(cap, high, near[2], MIN, 896, 1024)
-        finish(768, 896, nc.sync)
-        finish(896, 1024, nc.scalar)
+        finish(768, 896, nc.scalar)
+        finish(896, 1024, nc.sync)

@@ -22,8 +22,8 @@ LANES = 16
 BANK = 512
 PLANES = 4
 
-EARLY_ON_VECTOR = (896, 256)
-PIECES = ((256, 512), (512, 768), (768, 896), (896, 1024))
+EARLY_ON_VECTOR = (896, 512)
+PIECES = ((256, 384), (384, 512), (512, 768), (768, 896), (896, 1024))
 DIRECT = 256
 STRETCHES = ((0, 256), (256, 512), (512, 768), (768, 896), (896, 1024))
 
@@ -107,11 +107,12 @@ def tile_picked_median_none_e_kernel(tc, xT, w1_words, w1_scales, offs, pos1, po
             copy = nc.vector.tensor_copy if on_vector else nc.scalar.copy
             copy(out=ys[b][:, e0:e1], in_=acc)
 
-        lay(1, 256, 512, late[0][:])
+        lay(1, 256, 384, late[0][:])
         quantise(0, 256)
-        lay(1, 512, 768, late[1][:])
-        lay(1, 768, 896, late[2][:], False)
-        lay(1, 896, 1024, late[3][:], False)
+        lay(1, 384, 512, late[1][:])
+        lay(1, 512, 768, late[2][:])
+        lay(1, 768, 896, late[3][:], False)
+        lay(1, 896, 1024, late[4][:], False)
         for e0, e1 in STRETCHES[1:]:
             quantise(e0, e1)
         lower = [psum.tile([P, BANK], F32, name=f"lower{b}") for b in range(2)]
@@ -119,16 +120,18 @@ def tile_picked_median_none_e_kernel(tc, xT, w1_words, w1_scales, offs, pos1, po
             for b in range(2):
                 product(b, e0, e1, lower[b][:, e0:e1])
         empty(False, 0, 0, BANK, lower[0][:])
-        upper = psum.tile([P, BANK], F32, name="upper1")
+        third = psum.tile([P, BANK], F32, name="third1")[:, 0:256]
+        last = psum.tile([P, BANK], F32, name="last1")[:, 0:256]
         for i, (e0, e1) in enumerate(STRETCHES[2:]):
             acc = psum.tile([P, BANK], F32, name=f"upper0_{i}")[:, 0 : e1 - e0]
             product(0, e0, e1, acc)
             empty(i < 2, 0, e0, e1, acc)
             if i == 0:
-                product(1, e0, e1, upper[:, 0:256])
+                product(1, e0, e1, third)
         empty(False, 1, 0, BANK, lower[1][:])
-        product(1, 768, S, upper[:, 256:BANK])
-        empty(False, 1, BANK, S, upper[:])
+        empty(True, 1, 512, 768, third)
+        product(1, 768, S, last)
+        empty(False, 1, 768, S, last)
 
         near = [keep.tile([P, 2 * V], F32, name=f"near{d}") for d in range(3)]
         high, low, cap, med = (keep.tile([P, 2 * V], F32, name=what) for what in ("high", "low", "cap", "med"))

@@ -23,9 +23,11 @@ BANK = 512
 PLANES = 4
 
 EARLY_ON_VECTOR = (896, 512)
-PIECES = ((256, 384), (384, 512), (512, 768), (768, 896), (896, 1024))
 DIRECT = 256
-STRETCHES = ((0, 256), (256, 512), (512, 768), (768, 896), (896, 1024))
+UNIT = 128
+UNITS = (S - DIRECT) // UNIT
+LAID_BY_VECTOR = 4
+FIRST_ON_VECTOR = 896
 
 
 def tile_picked_median_none_e_kernel(tc, xT, w1_words, w1_scales, offs, pos1, pos2, pos3, out):
@@ -39,7 +41,6 @@ def tile_picked_median_none_e_kernel(tc, xT, w1_words, w1_scales, offs, pos1, po
         places = [keep.tile([P, V // LANES], U16, name=f"places{d}") for d in range(3)]
         w_words = keep.tile([P, 2 * N], U8, name="w_words", align_bytes=64)
         w_scales = keep.tile([P, N], U8, name="w_scales", align_bytes=64)
-
         nc.vector.memset(w_scales[:].bitcast(I32), 0)
 
         raws = [keep.tile([P, T], F32, name=f"raw{t}") for t in range(PLANES)]
@@ -64,8 +65,9 @@ def tile_picked_median_none_e_kernel(tc, xT, w1_words, w1_scales, offs, pos1, po
 
         quads = keep.tile([P, PLANES * S], BF16, name="quads", align_bytes=64)
         halves = quads[:].rearrange("p (j u t) -> p j u t", u=2, t=2)
+        slots = quads[:].rearrange("p (j t) -> p j t", t=PLANES)
 
-        def lay(u, e0, e1, pair, on_vector=True):
+        def lay(u, e0, e1, pair, on_vector):
             copy = nc.vector.tensor_copy if on_vector else nc.scalar.copy
             copy(out=halves[:, e0:e1, u, :], in_=pair.rearrange("p t j -> p j t"))
 
@@ -73,13 +75,16 @@ def tile_picked_median_none_e_kernel(tc, xT, w1_words, w1_scales, offs, pos1, po
         for t, share in enumerate(EARLY_ON_VECTOR):
             gather(True, early[:, t, 0:share], raws[t], entries(0, share))
             gather(False, early[:, t, share:S], raws[t], entries(share, S))
-        lay(0, 0, S, early[:])
-        slots = quads[:].rearrange("p (j t) -> p j t", t=PLANES)
-        late = [keep.tile([P, 2, e1 - e0], BF16, name=f"late{e0}") for e0, e1 in PIECES]
+        lay(0, 0, S, early[:], True)
+
+        def unit(i):
+            return DIRECT + UNIT * i, DIRECT + UNIT * (i + 1)
+
+        late = [keep.tile([P, 2, UNIT], BF16, name=f"late{i}") for i in range(UNITS)]
         for t in range(2):
             nc.vector.tensor_copy(out=slots[:, 0:DIRECT, 2 + t], in_=raws[2 + t][:].indirect(entries(0, DIRECT)))
-            for i, (e0, e1) in enumerate(PIECES):
-                gather(False, late[i][:, t, :], raws[2 + t], entries(e0, e1))
+            for i in range(UNITS):
+                gather(t == 0 and i < 2, late[i][:, t, :], raws[2 + t], entries(*unit(i)))
 
         codes = keep.tile([P, S], U32, name="codes", align_bytes=64)
         scales = keep.tile([P, S], U8, name="scales", align_bytes=64)
@@ -92,9 +97,20 @@ def tile_picked_median_none_e_kernel(tc, xT, w1_words, w1_scales, offs, pos1, po
                 in_=quads[:, PLANES * e0 : PLANES * e1],
             )
 
-        def product(b, e0, e1, acc):
+        spans = (((0, 512), (512, 768), (768, 896), (896, 1024)), ((0, 256), (256, 512), (512, 768), (768, 1024)))
+        banks = {}
+
+        def bank(b, i):
+            if (b, i) not in banks:
+                tag = "bank0_0" if (b, i) == (1, 2) else f"bank{b}_{i}"
+                banks[b, i] = psum.tile([P, BANK], F32, name=f"bank{b}_{i}", tag=tag)
+            return banks[b, i]
+
+        def product(b, e0, e1):
+            i = [s0 <= e0 < s1 for s0, s1 in spans[b]].index(True)
+            s0 = spans[b][i][0]
             nc.tensor.matmul_mx(
-                out=acc,
+                out=bank(b, i)[:, e0 - s0 : e1 - s0],
                 lhsT=w_words[:, 2 * P * b : 2 * P * (b + 1)].bitcast(FP4X4),
                 lhsT_scale=w_scales[:, P * b : P * (b + 1)],
                 rhs=codes[:, e0:e1].bitcast(FP8X4),
@@ -103,35 +119,34 @@ def tile_picked_median_none_e_kernel(tc, xT, w1_words, w1_scales, offs, pos1, po
                 stop=True,
             )
 
-        def empty(on_vector, b, e0, e1, acc):
+        def empty(on_vector, b, i):
+            e0, e1 = spans[b][i]
             copy = nc.vector.tensor_copy if on_vector else nc.scalar.copy
-            copy(out=ys[b][:, e0:e1], in_=acc)
+            copy(out=ys[b][:, e0:e1], in_=bank(b, i)[:, 0 : e1 - e0])
 
-        lay(1, 256, 384, late[0][:])
-        quantise(0, 256)
-        lay(1, 384, 512, late[1][:])
-        lay(1, 512, 768, late[2][:])
-        lay(1, 768, 896, late[3][:], False)
-        lay(1, 896, 1024, late[4][:], False)
-        for e0, e1 in STRETCHES[1:]:
-            quantise(e0, e1)
-        lower = [psum.tile([P, BANK], F32, name=f"lower{b}") for b in range(2)]
-        for e0, e1 in STRETCHES[:2]:
-            for b in range(2):
-                product(b, e0, e1, lower[b][:, e0:e1])
-        empty(False, 0, 0, BANK, lower[0][:])
-        third = psum.tile([P, BANK], F32, name="third1")[:, 0:256]
-        last = psum.tile([P, BANK], F32, name="last1")[:, 0:256]
-        for i, (e0, e1) in enumerate(STRETCHES[2:]):
-            acc = psum.tile([P, BANK], F32, name=f"upper0_{i}")[:, 0 : e1 - e0]
-            product(0, e0, e1, acc)
-            empty(i < 2, 0, e0, e1, acc)
-            if i == 0:
-                product(1, e0, e1, third)
-        empty(False, 1, 0, BANK, lower[1][:])
-        empty(True, 1, 512, 768, third)
-        product(1, 768, S, last)
-        empty(False, 1, 768, S, last)
+        for i in range(LAID_BY_VECTOR, UNITS):
+            lay(1, *unit(i), late[i][:], False)
+        lay(1, *unit(0), late[0][:], True)
+        quantise(0, DIRECT)
+        product(0, 0, DIRECT)
+        product(1, 0, DIRECT)
+        for i in range(UNITS):
+            if i + 1 < LAID_BY_VECTOR:
+                lay(1, *unit(i + 1), late[i + 1][:], True)
+            quantise(*unit(i))
+            product(0, *unit(i))
+            if i == 1:
+                product(1, 256, 512)
+        empty(False, 0, 0)
+        empty(True, 1, 0)
+        empty(False, 1, 1)
+        empty(True, 0, 1)
+        empty(True, 0, 2)
+        empty(False, 0, 3)
+        product(1, 512, 768)
+        product(1, 768, 1024)
+        empty(False, 1, 2)
+        empty(False, 1, 3)
 
         near = [keep.tile([P, 2 * V], F32, name=f"near{d}") for d in range(3)]
         high, low, cap, med = (keep.tile([P, 2 * V], F32, name=what) for what in ("high", "low", "cap", "med"))
@@ -149,9 +164,9 @@ def tile_picked_median_none_e_kernel(tc, xT, w1_words, w1_scales, offs, pos1, po
             queue.dma_start(out=out[P * b : P * (b + 1), v0 : v0 + c1 - c0], in_=med[:, c0:c1])
 
         fetch(True, 0, 0, 512)
-        fetch(True, 0, 512, 896)
+        fetch(True, 0, 512, FIRST_ON_VECTOR)
         fetch(False, 1, 0, 512)
-        fetch(False, 0, 896, 1024)
+        fetch(False, 0, FIRST_ON_VECTOR, 1024)
         fetch(False, 1, 512, 1024)
         fetch(False, 2, 0, 512)
         fetch(False, 2, 512, 768)

@@ -22,12 +22,11 @@ LANES = 16
 BANK = 512
 PLANES = 4
 
-EARLY_ON_VECTOR = (896, 512)
+EARLY = ((0, 384), (384, 896), (896, 1024))
 DIRECT = 256
 UNIT = 128
 UNITS = (S - DIRECT) // UNIT
 LAID_BY_VECTOR = 4
-FIRST_ON_VECTOR = 896
 
 
 def tile_picked_median_none_e_kernel(tc, xT, w1_words, w1_scales, offs, pos1, pos2, pos3, out):
@@ -43,7 +42,7 @@ def tile_picked_median_none_e_kernel(tc, xT, w1_words, w1_scales, offs, pos1, po
         w_scales = keep.tile([P, N], U8, name="w_scales", align_bytes=64)
         nc.vector.memset(w_scales[:].bitcast(I32), 0)
 
-        raws = [keep.tile([P, T], F32, name=f"raw{t}") for t in range(PLANES)]
+        raws = [keep.tile([P, T], F32, name=f"raw{t}", align_bytes=256) for t in range(PLANES)]
         nc.sync.dma_start(out=raws[0][:], in_=x_rows[:, 0, :])
         nc.sync.dma_start(picks[:], offs)
         for t in range(1, PLANES):
@@ -71,11 +70,12 @@ def tile_picked_median_none_e_kernel(tc, xT, w1_words, w1_scales, offs, pos1, po
             copy = nc.vector.tensor_copy if on_vector else nc.scalar.copy
             copy(out=halves[:, e0:e1, u, :], in_=pair.rearrange("p t j -> p j t"))
 
-        early = keep.tile([P, 2, S], BF16, name="early")
-        for t, share in enumerate(EARLY_ON_VECTOR):
-            gather(True, early[:, t, 0:share], raws[t], entries(0, share))
-            gather(False, early[:, t, share:S], raws[t], entries(share, S))
-        lay(0, 0, S, early[:], True)
+        early = [keep.tile([P, 2, e1 - e0], BF16, name=f"early{e0}") for e0, e1 in EARLY]
+        for t in range(2):
+            for i, (e0, e1) in enumerate(EARLY):
+                gather(i < 2 - t, early[i][:, t, :], raws[t], entries(e0, e1))
+        for i, (e0, e1) in enumerate(EARLY):
+            lay(0, e0, e1, early[i][:], True)
 
         def unit(i):
             return DIRECT + UNIT * i, DIRECT + UNIT * (i + 1)
@@ -84,7 +84,7 @@ def tile_picked_median_none_e_kernel(tc, xT, w1_words, w1_scales, offs, pos1, po
         for t in range(2):
             nc.vector.tensor_copy(out=slots[:, 0:DIRECT, 2 + t], in_=raws[2 + t][:].indirect(entries(0, DIRECT)))
             for i in range(UNITS):
-                gather(t == 0 and i < 2, late[i][:, t, :], raws[2 + t], entries(*unit(i)))
+                gather(t == 0 and i < 1, late[i][:, t, :], raws[2 + t], entries(*unit(i)))
 
         codes = keep.tile([P, S], U32, name="codes", align_bytes=64)
         scales = keep.tile([P, S], U8, name="scales", align_bytes=64)
@@ -148,36 +148,38 @@ def tile_picked_median_none_e_kernel(tc, xT, w1_words, w1_scales, offs, pos1, po
         empty(False, 1, 2)
         empty(False, 1, 3)
 
-        near = [keep.tile([P, 2 * V], F32, name=f"near{d}") for d in range(3)]
-        high, low, cap, med = (keep.tile([P, 2 * V], F32, name=what) for what in ("high", "low", "cap", "med"))
+        shared = keep.tile([P, 896], F32, name="shared")
+        own = [keep.tile([P, V], F32, name=f"own{i}") for i in range(4)]
+        near = ((own[0][:], shared[:, 384:896], own[1][:]), (shared[:, 0:V], own[2][:], own[3][:]))
+        high, low, cap, med = ([keep.tile([P, V], F32, name=f"{what}{b}", align_bytes=256) for b in range(2)] for what in ("high", "low", "cap", "med"))
 
-        def fetch(on_vector, d, c0, c1):
-            b, v0 = divmod(c0, V)
-            gather(on_vector, near[d][:, c0:c1], ys[b], places[d][:, v0 // LANES : (v0 + c1 - c0) // LANES])
+        def fetch(on_vector, b, d, v0, v1):
+            gather(on_vector, near[b][d][:, v0:v1], ys[b], places[d][:, v0 // LANES : v1 // LANES])
 
-        def step(result, left, right, op, c0, c1):
-            nc.vector.tensor_tensor(result[:, c0:c1], left[:, c0:c1], right[:, c0:c1], op)
+        def step(result, left, right, op, v0, v1):
+            nc.vector.tensor_tensor(result[:, v0:v1], left[:, v0:v1], right[:, v0:v1], op)
 
-        def finish(c0, c1, queue):
-            step(med, low, cap, MAX, c0, c1)
-            b, v0 = divmod(c0, V)
-            queue.dma_start(out=out[P * b : P * (b + 1), v0 : v0 + c1 - c0], in_=med[:, c0:c1])
+        def store(queue, b, v0, v1):
+            queue.dma_start(out=out[P * b : P * (b + 1), v0:v1], in_=med[b][:, v0:v1])
 
-        fetch(True, 0, 0, 512)
-        fetch(True, 0, 512, FIRST_ON_VECTOR)
-        fetch(False, 1, 0, 512)
-        fetch(False, 0, FIRST_ON_VECTOR, 1024)
-        fetch(False, 1, 512, 1024)
-        fetch(False, 2, 0, 512)
-        fetch(False, 2, 512, 768)
-        fetch(False, 2, 768, 1024)
-        for c0 in (0, 512):
-            step(high, near[0], near[1], MAX, c0, c0 + 512)
-            step(low, near[0], near[1], MIN, c0, c0 + 512)
-        step(cap, high, near[2], MIN, 0, 512)
-        step(cap, high, near[2], MIN, 512, 768)
-        finish(0, 512, nc.sync)
-        step(cap, high, near[2], MIN, 768, 1024)
-        finish(512, 768, nc.sync)
-        finish(768, 896, nc.scalar)
-        finish(896, 1024, nc.sync)
+        fetch(True, 0, 0, 0, V)
+        fetch(True, 1, 0, 128, 384)
+        fetch(False, 0, 1, 0, V)
+        fetch(False, 0, 2, 0, V)
+        fetch(False, 1, 0, 0, 128)
+        fetch(False, 1, 1, 0, V)
+        fetch(False, 1, 2, 0, 320)
+        fetch(False, 1, 2, 320, V)
+        step(high[0], near[0][0], near[0][1], MAX, 0, V)
+        step(low[0], near[0][0], near[0][1], MIN, 0, V)
+        step(cap[0], high[0], near[0][2], MIN, 0, V)
+        fetch(True, 1, 0, 384, V)
+        step(med[0], low[0], cap[0], MAX, 0, V)
+        step(high[1], near[1][0], near[1][1], MAX, 0, V)
+        step(low[1], near[1][0], near[1][1], MIN, 0, V)
+        for v0, v1 in ((0, 128), (128, 320), (320, V)):
+            step(cap[1], high[1], near[1][2], MIN, v0, v1)
+        store(nc.scalar, 0, 0, V)
+        for queue, v0, v1 in ((nc.sync, 0, 128), (nc.scalar, 128, 320), (nc.sync, 320, V)):
+            step(med[1], low[1], cap[1], MAX, v0, v1)
+            store(queue, 1, v0, v1)

from contextlib import ExitStack

import concourse.mybir as mybir

K, T, S, V, N = 512, 2048, 1024, 512, 256
FLOPS = 2 * K * S * N

F32 = mybir.dt.float32
BF16 = mybir.dt.bfloat16
I32 = mybir.dt.int32
U32 = mybir.dt.uint32
U16 = mybir.dt.uint16
U8 = mybir.dt.uint8
FP8X4 = mybir.dt.float8_e4m3fn_x4
FP4X4 = mybir.dt.float4_e2m1fn_x4
MAX = mybir.AluOpType.max
MIN = mybir.AluOpType.min
COPY = mybir.ActivationFunctionType.Copy

P = 128
LANES = 16
BANK = 512
PLANES = 4

EARLY = ((0, 384), (384, 896), (896, 1024))
DIRECT = 256
UNIT = 128
UNITS = (S - DIRECT) // UNIT
LAID_BY_VECTOR = 4


def tile_picked_median_none_e_kernel(tc, xT, w1_words, w1_scales, offs, pos1, pos2, pos3, out):
    nc = tc.nc
    with ExitStack() as ctx:
        keep = ctx.enter_context(tc.tile_pool(name="keep", bufs=1))
        psum = ctx.enter_context(tc.psum_pool(name="psum", bufs=1))

        x_rows = xT.rearrange("(p t) n -> p t n", t=PLANES)
        picks = keep.tile([P, S // LANES], U16, name="picks")
        places = [keep.tile([P, V // LANES], U16, name=f"places{d}") for d in range(3)]
        w_words = keep.tile([P, 2 * N], U8, name="w_words", align_bytes=64)
        w_scales = keep.tile([P, N], U8, name="w_scales", align_bytes=64)
        nc.vector.memset(w_scales[:].bitcast(I32), 0)

        raws = [keep.tile([P, T], F32, name=f"raw{t}", align_bytes=256) for t in range(PLANES)]
        nc.sync.dma_start(out=raws[0][:], in_=x_rows[:, 0, :])
        nc.sync.dma_start(picks[:], offs)
        for t in range(1, PLANES):
            nc.sync.dma_start(out=raws[t][:], in_=x_rows[:, t, :])
        nc.sync.dma_start(out=w_words[:], in_=w1_words[0])
        for q in range(4):
            nc.sync.dma_start(out=w_scales[32 * q : 32 * q + 4, :].bitcast(I32), in_=w1_scales[0, 4 * q : 4 * q + 4, :].bitcast(I32))
        for place, pos in zip(places, (pos1, pos2, pos3)):
            nc.sync.dma_start(place[:], pos)

        def gather(on_vector, got, window, offsets):
            if on_vector:
                nc.vector.tensor_copy(out=got, in_=window[:].indirect(offsets))
            else:
                nc.scalar.activation(got, window[:].indirect(offsets), COPY)

        def entries(e0, e1):
            return picks[:, e0 // LANES : e1 // LANES]

        quads = keep.tile([P, PLANES * S], BF16, name="quads", align_bytes=64)
        halves = quads[:].rearrange("p (j u t) -> p j u t", u=2, t=2)
        slots = quads[:].rearrange("p (j t) -> p j t", t=PLANES)

        def lay(u, e0, e1, pair, on_vector):
            copy = nc.vector.tensor_copy if on_vector else nc.scalar.copy
            copy(out=halves[:, e0:e1, u, :], in_=pair.rearrange("p t j -> p j t"))

        early = [keep.tile([P, 2, e1 - e0], BF16, name=f"early{e0}") for e0, e1 in EARLY]
        for t in range(2):
            for i, (e0, e1) in enumerate(EARLY):
                gather(i < 2 - t, early[i][:, t, :], raws[t], entries(e0, e1))
        for i, (e0, e1) in enumerate(EARLY):
            lay(0, e0, e1, early[i][:], True)

        def unit(i):
            return DIRECT + UNIT * i, DIRECT + UNIT * (i + 1)

        late = [keep.tile([P, 2, UNIT], BF16, name=f"late{i}") for i in range(UNITS)]
        for t in range(2):
            nc.vector.tensor_copy(out=slots[:, 0:DIRECT, 2 + t], in_=raws[2 + t][:].indirect(entries(0, DIRECT)))
            for i in range(UNITS):
                gather(t == 0 and i < 1, late[i][:, t, :], raws[2 + t], entries(*unit(i)))

        codes = keep.tile([P, S], U32, name="codes", align_bytes=64)
        scales = keep.tile([P, S], U8, name="scales", align_bytes=64)
        ys = [keep.tile([P, S], F32, name=f"y{b}") for b in range(2)]

        def quantise(e0, e1):
            nc.vector.quantize_mx(
                out=codes[:, e0:e1].bitcast(FP8X4),
                scales=scales[:, e0:e1],
                in_=quads[:, PLANES * e0 : PLANES * e1],
            )

        spans = (((0, 512), (512, 768), (768, 896), (896, 1024)), ((0, 256), (256, 512), (512, 768), (768, 1024)))
        banks = {}

        def bank(b, i):
            if (b, i) not in banks:
                tag = "bank0_0" if (b, i) == (1, 2) else f"bank{b}_{i}"
                banks[b, i] = psum.tile([P, BANK], F32, name=f"bank{b}_{i}", tag=tag)
            return banks[b, i]

        def product(b, e0, e1):
            i = [s0 <= e0 < s1 for s0, s1 in spans[b]].index(True)
            s0 = spans[b][i][0]
            nc.tensor.matmul_mx(
                out=bank(b, i)[:, e0 - s0 : e1 - s0],
                lhsT=w_words[:, 2 * P * b : 2 * P * (b + 1)].bitcast(FP4X4),
                lhsT_scale=w_scales[:, P * b : P * (b + 1)],
                rhs=codes[:, e0:e1].bitcast(FP8X4),
                rhs_scale=scales[:, e0:e1],
                start=True,
                stop=True,
            )

        def empty(on_vector, b, i):
            e0, e1 = spans[b][i]
            copy = nc.vector.tensor_copy if on_vector else nc.scalar.copy
            copy(out=ys[b][:, e0:e1], in_=bank(b, i)[:, 0 : e1 - e0])

        for i in range(LAID_BY_VECTOR, UNITS):
            lay(1, *unit(i), late[i][:], False)
        lay(1, *unit(0), late[0][:], True)
        quantise(0, DIRECT)
        product(0, 0, DIRECT)
        product(1, 0, DIRECT)
        for i in range(UNITS):
            if i + 1 < LAID_BY_VECTOR:
                lay(1, *unit(i + 1), late[i + 1][:], True)
            quantise(*unit(i))
            product(0, *unit(i))
            if i == 1:
                product(1, 256, 512)
        empty(False, 0, 0)
        empty(True, 1, 0)
        empty(False, 1, 1)
        empty(True, 0, 1)
        empty(True, 0, 2)
        empty(False, 0, 3)
        product(1, 512, 768)
        product(1, 768, 1024)
        empty(False, 1, 2)
        empty(False, 1, 3)

        shared = keep.tile([P, 896], F32, name="shared")
        own = [keep.tile([P, V], F32, name=f"own{i}") for i in range(4)]
        near = ((own[0][:], shared[:, 384:896], own[1][:]), (shared[:, 0:V], own[2][:], own[3][:]))
        high, low, cap, med = ([keep.tile([P, V], F32, name=f"{what}{b}", align_bytes=256) for b in range(2)] for what in ("high", "low", "cap", "med"))

        def fetch(on_vector, b, d, v0, v1):
            gather(on_vector, near[b][d][:, v0:v1], ys[b], places[d][:, v0 // LANES : v1 // LANES])

        def step(result, left, right, op, v0, v1):
            nc.vector.tensor_tensor(result[:, v0:v1], left[:, v0:v1], right[:, v0:v1], op)

        def store(queue, b, v0, v1):
            queue.dma_start(out=out[P * b : P * (b + 1), v0:v1], in_=med[b][:, v0:v1])

        fetch(True, 0, 0, 0, V)
        fetch(True, 1, 0, 128, 384)
        fetch(False, 0, 1, 0, V)
        fetch(False, 0, 2, 0, V)
        fetch(False, 1, 0, 0, 128)
        fetch(False, 1, 1, 0, V)
        fetch(False, 1, 2, 0, 320)
        fetch(False, 1, 2, 320, V)
        step(high[0], near[0][0], near[0][1], MAX, 0, V)
        step(low[0], near[0][0], near[0][1], MIN, 0, V)
        step(cap[0], high[0], near[0][2], MIN, 0, V)
        fetch(True, 1, 0, 384, V)
        step(med[0], low[0], cap[0], MAX, 0, V)
        step(high[1], near[1][0], near[1][1], MAX, 0, V)
        step(low[1], near[1][0], near[1][1], MIN, 0, V)
        for v0, v1 in ((0, 128), (128, 320), (320, V)):
            step(cap[1], high[1], near[1][2], MIN, v0, v1)
        store(nc.scalar, 0, 0, V)
        for queue, v0, v1 in ((nc.sync, 0, 128), (nc.scalar, 128, 320), (nc.sync, 320, V)):
            step(med[1], low[1], cap[1], MAX, v0, v1)
            store(queue, 1, v0, v1)
